import numpy as np
import ml_dtypes


def mxq(x, axis, fmt="e4m3"):
    dtype, down = {"e4m3": (ml_dtypes.float8_e4m3fn, 7), "e5m2": (ml_dtypes.float8_e5m2, 14)}[fmt]
    v = np.moveaxis(np.asarray(x, np.float32).astype(ml_dtypes.bfloat16).astype(np.float64), axis, -1)
    blocks = v.reshape(v.shape[:-1] + (-1, 32))
    amax = np.abs(blocks).max(-1, keepdims=True)
    byte = np.maximum(np.where(amax > 0, np.frexp(amax)[1] - 1 + 127, 0) - down, 1)
    scale = np.exp2(byte - 127.0)
    codes = (blocks / scale).astype(np.float32).astype(dtype).astype(np.float64)
    return np.moveaxis((codes * scale).reshape(v.shape), -1, axis)


WIDE = False


def mx_kscale(k):
    if not WIDE:
        return np.ones(k)
    levels = np.array([10, -10, 5, -5, 0])
    if k % 512:
        return np.exp2(np.random.permutation(np.resize(levels, k // 32))).repeat(32)
    a = np.empty((k // 512, 16))
    for p in range(k // 512):
        a[p, :8] = np.random.permutation(np.resize(levels, 8))
        for g in range(8):
            far = levels[np.abs(levels - a[p, g]) >= 10]
            a[p, g + 8] = far[np.random.randint(len(far))]
    return np.exp2(a.ravel()).repeat(32)


def f64(x):
    return np.asarray(x).astype(np.float64)


def striped(idx):
    return np.tile(idx.reshape(-1, 16).T, (8, 1)).astype(np.uint16)


def unstriped(offs):
    return offs[:16].T.reshape(-1).astype(np.int64)


def pack_weight(w):
    k, n = w.shape
    w = f64(np.asarray(w, np.float32).astype(ml_dtypes.bfloat16)).reshape(k // 32, 32, n)
    amax = np.abs(w).max(1)
    byte = np.clip(np.where(amax > 0, np.frexp(amax)[1] - 1 + 127 - 7, 1), 1, 254)
    scaled = (w * np.exp2(127.0 - byte)[:, None, :]).reshape(k, n).astype(np.float32)
    words = np.ascontiguousarray(scaled.reshape(k // 512, 128, 4, n).transpose(0, 1, 3, 2)).astype(ml_dtypes.float8_e4m3fn).view(np.uint8)
    return words, np.ascontiguousarray(byte.astype(np.uint8).reshape(k // 512, 16, n))


def unpack_weight(words, scales):
    g, p, n, _ = words.shape
    vals = np.ascontiguousarray(words).view(ml_dtypes.float8_e4m3fn).astype(np.float64) * np.repeat(np.exp2(scales.astype(np.float64) - 127.0), 8, axis=1)[..., None]
    return vals.transpose(0, 1, 3, 2).reshape(g * 512, n)


K, T, S, H = 512, 2048, 512, 512


def setup_inputs():
    n = np.random.standard_normal
    s = mx_kscale(K)[:, None]
    u = mx_kscale(S)
    packed_xT = pack_weight(n((K, T)) * s)
    return {
        "x_words": packed_xT[0],
        "x_scales": packed_xT[1],
        "wa": (n((K, H)) / np.sqrt(K) / s).astype(np.float32),
        "wb": (n((K, H)) / np.sqrt(K) / s).astype(np.float32),
        "gt": (np.random.uniform(0.5, 1.5, (S, 1)) * u[:, None]).astype(np.float32),
        "gi": (np.random.uniform(0.5, 1.5, (S, 1)) / u[:, None]).astype(np.float32),
        "offs": striped(np.random.permutation(T)[:S]),
    }


def reference(x_words, x_scales, wa, wb, gt, gi, offs):
    xq = unpack_weight(x_words, x_scales)[:, unstriped(offs)]
    a = xq.T @ mxq(f64(wa), 0, "e4m3")
    z = f64(gt) * a
    b = xq.T @ mxq(f64(wb), 0, "e4m3")
    z2 = f64(gi) * b
    return 0.0625 * ((mxq(z, 0, "e4m3").T @ mxq(z2, 0, "e4m3")))

@@ -1,0 +1,139 @@
+from contextlib import ExitStack
+
+import concourse.mybir as mybir
+
+K, T, S, H = 512, 2048, 512, 512
+FLOPS = 2 * K * S * H * 2 + 2 * S * H * H
+
+F32 = mybir.dt.float32
+BF16 = mybir.dt.bfloat16
+I32 = mybir.dt.int32
+U32 = mybir.dt.uint32
+U16 = mybir.dt.uint16
+U8 = mybir.dt.uint8
+FP8X4 = mybir.dt.float8_e4m3fn_x4
+MULT = mybir.AluOpType.mult
+COPY = mybir.ActivationFunctionType.Copy
+
+P = 128
+PACK = 4
+CH = 128
+NCH = H // CH
+B_LOADS = (128, 128, 256)
+A_LOADS = (256, 256)
+
+
+def tile_picked_bilpool_none_p_kernel(tc, x_words, x_scales, wa, wb, gt, gi, offs, out):
+    nc = tc.nc
+    with ExitStack() as ctx:
+        keep = ctx.enter_context(tc.tile_pool(name="keep", bufs=1))
+        psum = ctx.enter_context(tc.psum_pool(name="psum", bufs=1))
+
+        offsets = keep.tile([P, S // 16], U16, name="offsets")
+        scale_table = keep.tile([P, T], U8, name="scale_table", align_bytes=64)
+        word_table = keep.tile([P, T], I32, name="word_table", align_bytes=64)
+        gi_sb = keep.tile([P, PACK], F32, name="gi_sb")
+        gt_sb = keep.tile([P, PACK], F32, name="gt_sb")
+
+        nc.vector.memset(scale_table[:].bitcast(I32), 0)
+        nc.sync.dma_start(offsets[:], offs)
+        nc.sync.dma_start(gi_sb[:], gi.rearrange("(p t) o -> p (t o)", t=PACK))
+        nc.sync.dma_start(gt_sb[:], gt.rearrange("(p t) o -> p (t o)", t=PACK))
+        for q in range(4):
+            nc.sync.dma_start(scale_table[32 * q : 32 * q + 4, :].bitcast(I32), x_scales[0, 4 * q : 4 * q + 4, :].bitcast(I32))
+        nc.sync.dma_start(word_table[:], x_words[0].rearrange("p n t -> p (n t)").bitcast(I32))
+
+        def load_weights(w, widths, label):
+            pieces = []
+            c0 = 0
+            rows = w.rearrange("(p t) n -> p t n", t=PACK)
+            for width in widths:
+                raw = keep.tile([P, PACK, width], F32, name="%s_raw%d" % (label, c0))
+                nc.sync.dma_start(raw[:], rows[:, :, c0 : c0 + width])
+                for c in range(0, width, CH):
+                    pieces.append(raw[:, :, c : c + CH])
+                c0 = c0 + width
+            return pieces
+
+        raw_chunks = load_weights(wb, B_LOADS, "wb") + load_weights(wa, A_LOADS, "wa")
+
+        picked_bytes = keep.tile([P, S], U8, name="picked_bytes", align_bytes=64)
+        x_planes = keep.tile([P, PACK, P], U8, name="x_planes", align_bytes=64)
+        x_codes = keep.tile([P, PACK, P], U32, name="x_codes", align_bytes=64)
+        nc.vector.tensor_copy(picked_bytes[:], scale_table[:].indirect(offsets[:]))
+        nc.vector.tensor_copy(x_planes[:].rearrange("p t m -> p m t"), picked_bytes[:].rearrange("p (m t) -> p m t", t=PACK))
+        nc.vector.tensor_copy(x_codes[:].rearrange("p t m -> p m t"), word_table[:].bitcast(U32).indirect(offsets[:]))
+
+        z2_codes = keep.tile([P, H], U32, name="z2_codes", align_bytes=64)
+        z2_planes = keep.tile([P, H], U8, name="z2_planes", align_bytes=64)
+
+        w_q = {}
+        z_bf = {}
+
+        def cast_w(c):
+            grouped = keep.tile([P, CH, PACK], BF16, name="w_bf%d" % c, align_bytes=64)
+            nc.scalar.copy(grouped[:].rearrange("p (c i) t -> p c t i", i=4), raw_chunks[c].rearrange("p t (c i) -> p c t i", i=4))
+            return grouped
+
+        def quant_w(c, grouped):
+            codes = keep.tile([P, CH], U32, name="w_codes%d" % c, align_bytes=64)
+            planes = keep.tile([P, CH], U8, name="w_planes%d" % c, align_bytes=64)
+            nc.vector.quantize_mx(out=codes[:].bitcast(FP8X4), scales=planes[:], in_=grouped[:].rearrange("p n t -> p (n t)"))
+            w_q[c] = (codes, planes)
+
+        def project(c):
+            codes, planes = w_q[c]
+            acc = psum.tile([P, PACK, CH], F32, name="proj%d" % (c % 4))
+            for t in range(PACK):
+                nc.tensor.matmul_mx(out=acc[:, t, :], lhsT=x_codes[:, t, :].bitcast(FP8X4), lhsT_scale=x_planes[:, t, :],
+                                    rhs=codes[:].bitcast(FP8X4), rhs_scale=planes[:], start=True, stop=True)
+            return acc
+
+        def weigh(c, acc):
+            gate = gi_sb if c < NCH else gt_sb
+            zb = keep.tile([P, CH, PACK], BF16, name="z_bf%d" % c, align_bytes=64)
+            nc.vector.tensor_tensor(zb[:], acc[:].rearrange("p t n -> p n t"), gate[:].unsqueeze(1).to_broadcast([P, CH, PACK]), MULT)
+            z_bf[c] = zb
+
+        def quant_z(c):
+            src = z_bf[c][:].rearrange("p n t -> p (n t)")
+            if c < NCH:
+                cols = slice(c * CH, (c + 1) * CH)
+                nc.vector.quantize_mx(out=z2_codes[:, cols].bitcast(FP8X4), scales=z2_planes[:, cols], in_=src)
+                return
+            i = c - NCH
+            codes = keep.tile([P, CH], U32, name="z_codes%d" % i, align_bytes=64)
+            planes = keep.tile([P, CH], U8, name="z_planes%d" % i, align_bytes=64)
+            nc.vector.quantize_mx(out=codes[:].bitcast(FP8X4), scales=planes[:], in_=src)
+            rows = slice(i * CH, (i + 1) * CH)
+            if i < 2:
+                pooled = psum.tile([P, H], F32, name="pooled%d" % i)
+                nc.tensor.matmul_mx(out=pooled[:], lhsT=codes[:].bitcast(FP8X4), lhsT_scale=planes[:],
+                                    rhs=z2_codes[:].bitcast(FP8X4), rhs_scale=z2_planes[:], start=True, stop=True)
+                res = keep.tile([P, H], F32, name="res%d" % i)
+                nc.scalar.activation(res[:], pooled[:], COPY, scale=0.0625)
+                nc.sync.dma_start(out[rows, :], res[:])
+                return
+            for h in range(2):
+                cols = slice(h * 256, (h + 1) * 256)
+                pooled = psum.tile([P, 256], F32, name=("pooled%d" % (2 + h)) if i == 2 else ("proj%d" % h))
+                nc.tensor.matmul_mx(out=pooled[:], lhsT=codes[:].bitcast(FP8X4), lhsT_scale=planes[:],
+                                    rhs=z2_codes[:, cols].bitcast(FP8X4), rhs_scale=z2_planes[:, cols], start=True, stop=True)
+                res = keep.tile([P, 256], F32, name="res%d_%d" % (i, h))
+                if h == 0:
+                    nc.scalar.activation(res[:], pooled[:], COPY, scale=0.0625)
+                    nc.sync.dma_start(out[rows, cols], res[:])
+                else:
+                    nc.vector.tensor_scalar(res[:], pooled[:], 0.0625, None, MULT)
+                    nc.sync.dma_start(out[rows, cols], res[:])
+
+        n = 2 * NCH
+        accs = {}
+        for step in range(n + 2):
+            if step < n:
+                quant_w(step, cast_w(step))
+                accs[step] = project(step)
+            if 1 <= step <= n:
+                weigh(step - 1, accs[step - 1])
+            if step >= 2:
+                quant_z(step - 2)

@@ -19,7 +19,7 @@ P = 128
 PACK = 4
 CH = 128
 NCH = H // CH
-B_LOADS = (128, 128, 256)
+B_LOADS = (128, 128, 128, 128)
 A_LOADS = (256, 256)
 
 
@@ -32,13 +32,18 @@ def tile_picked_bilpool_none_p_kernel(tc, x_words, x_scales, wa, wb, gt, gi, off
         offsets = keep.tile([P, S // 16], U16, name="offsets")
         scale_table = keep.tile([P, T], U8, name="scale_table", align_bytes=64)
         word_table = keep.tile([P, T], I32, name="word_table", align_bytes=64)
-        gi_sb = keep.tile([P, PACK], F32, name="gi_sb")
-        gt_sb = keep.tile([P, PACK], F32, name="gt_sb")
+        gi_sb = keep.tile([P, 8], F32, name="gi_sb")
+        gt_sb = keep.tile([P, 8], F32, name="gt_sb")
+
+        def load_gate(tile, gate):
+            runs = gate.rearrange("(g e) o -> g (e o)", e=8)
+            for r in range(2):
+                nc.sync.dma_start(tile[r:P:2, 0:7], runs[:, r : r + 7])
+
 
         nc.vector.memset(scale_table[:].bitcast(I32), 0)
         nc.sync.dma_start(offsets[:], offs)
-        nc.sync.dma_start(gi_sb[:], gi.rearrange("(p t) o -> p (t o)", t=PACK))
-        nc.sync.dma_start(gt_sb[:], gt.rearrange("(p t) o -> p (t o)", t=PACK))
+        load_gate(gi_sb, gi)
         for q in range(4):
             nc.sync.dma_start(scale_table[32 * q : 32 * q + 4, :].bitcast(I32), x_scales[0, 4 * q : 4 * q + 4, :].bitcast(I32))
         nc.sync.dma_start(word_table[:], x_words[0].rearrange("p n t -> p (n t)").bitcast(I32))
@@ -55,14 +60,16 @@ def tile_picked_bilpool_none_p_kernel(tc, x_words, x_scales, wa, wb, gt, gi, off
                 c0 = c0 + width
             return pieces
 
-        raw_chunks = load_weights(wb, B_LOADS, "wb") + load_weights(wa, A_LOADS, "wa")
+        raw_chunks = load_weights(wb, B_LOADS, "wb")
+        load_gate(gt_sb, gt)
+        raw_chunks = raw_chunks + load_weights(wa, A_LOADS, "wa")
 
         picked_bytes = keep.tile([P, S], U8, name="picked_bytes", align_bytes=64)
         x_planes = keep.tile([P, PACK, P], U8, name="x_planes", align_bytes=64)
         x_codes = keep.tile([P, PACK, P], U32, name="x_codes", align_bytes=64)
         nc.vector.tensor_copy(picked_bytes[:], scale_table[:].indirect(offsets[:]))
-        nc.vector.tensor_copy(x_planes[:].rearrange("p t m -> p m t"), picked_bytes[:].rearrange("p (m t) -> p m t", t=PACK))
-        nc.vector.tensor_copy(x_codes[:].rearrange("p t m -> p m t"), word_table[:].bitcast(U32).indirect(offsets[:]))
+        nc.vector.tensor_copy(x_planes[:].rearrange("p t (g r) -> p t g r", r=2), picked_bytes[:].rearrange("p (g t r) -> p t g r", t=PACK, r=2))
+        nc.vector.tensor_copy(x_codes[:].rearrange("p t (g r) -> p g t r", r=2), word_table[:].bitcast(U32).indirect(offsets[:]))
 
         z2_codes = keep.tile([P, H], U32, name="z2_codes", align_bytes=64)
         z2_planes = keep.tile([P, H], U8, name="z2_planes", align_bytes=64)
@@ -92,7 +99,7 @@ def tile_picked_bilpool_none_p_kernel(tc, x_words, x_scales, wa, wb, gt, gi, off
         def weigh(c, acc):
             gate = gi_sb if c < NCH else gt_sb
             zb = keep.tile([P, CH, PACK], BF16, name="z_bf%d" % c, align_bytes=64)
-            nc.vector.tensor_tensor(zb[:], acc[:].rearrange("p t n -> p n t"), gate[:].unsqueeze(1).to_broadcast([P, CH, PACK]), MULT)
+            nc.vector.tensor_tensor(zb[:], acc[:].rearrange("p t n -> p n t"), gate[:, 0:7:2].unsqueeze(1).to_broadcast([P, CH, PACK]), MULT)
             z_bf[c] = zb
 
         def quant_z(c):
@@ -129,11 +136,11 @@ def tile_picked_bilpool_none_p_kernel(tc, x_words, x_scales, wa, wb, gt, gi, off
 
         n = 2 * NCH
         accs = {}
-        for step in range(n + 2):
+        for step in range(n + 3):
             if step < n:
                 quant_w(step, cast_w(step))
                 accs[step] = project(step)
-            if 1 <= step <= n:
-                weigh(step - 1, accs[step - 1])
-            if step >= 2:
-                quant_z(step - 2)
+            if 2 <= step < n + 2:
+                weigh(step - 2, accs[step - 2])
+            if step >= 3:
+                quant_z(step - 3)

@@ -41,28 +41,32 @@ def tile_picked_bilpool_none_p_kernel(tc, x_words, x_scales, wa, wb, gt, gi, off
                 nc.sync.dma_start(tile[r:P:2, 0:7], runs[:, r : r + 7])
 
 
+        raw_chunks = {}
+
+        def load_weights(w, first, c0, width):
+            raw = keep.tile([P, PACK, width], F32, name="raw%d" % (first + c0 // CH))
+            nc.sync.dma_start(raw[:], w.rearrange("(p t) n -> p t n", t=PACK)[:, :, c0 : c0 + width])
+            for c in range(0, width, CH):
+                raw_chunks[first + (c0 + c) // CH] = raw[:, :, c : c + CH]
+
+        def load_scales(q, eng):
+            eng.dma_start(scale_table[32 * q : 32 * q + 4, :].bitcast(I32), x_scales[0, 4 * q : 4 * q + 4, :].bitcast(I32))
+
         nc.vector.memset(scale_table[:].bitcast(I32), 0)
         nc.sync.dma_start(offsets[:], offs)
         load_gate(gi_sb, gi)
-        for q in range(4):
-            nc.sync.dma_start(scale_table[32 * q : 32 * q + 4, :].bitcast(I32), x_scales[0, 4 * q : 4 * q + 4, :].bitcast(I32))
+        load_scales(0, nc.sync)
+        load_scales(1, nc.sync)
+        load_scales(2, nc.scalar)
+        load_scales(3, nc.scalar)
         nc.sync.dma_start(word_table[:], x_words[0].rearrange("p n t -> p (n t)").bitcast(I32))
-
-        def load_weights(w, widths, label):
-            pieces = []
-            c0 = 0
-            rows = w.rearrange("(p t) n -> p t n", t=PACK)
-            for width in widths:
-                raw = keep.tile([P, PACK, width], F32, name="%s_raw%d" % (label, c0))
-                nc.sync.dma_start(raw[:], rows[:, :, c0 : c0 + width])
-                for c in range(0, width, CH):
-                    pieces.append(raw[:, :, c : c + CH])
-                c0 = c0 + width
-            return pieces
-
-        raw_chunks = load_weights(wb, B_LOADS, "wb")
+        load_weights(wb, 0, 0, 128)
+        load_weights(wb, 0, 128, 128)
+        load_weights(wb, 0, 256, 128)
+        load_weights(wb, 0, 384, 128)
         load_gate(gt_sb, gt)
-        raw_chunks = raw_chunks + load_weights(wa, A_LOADS, "wa")
+        load_weights(wa, 4, 0, 256)
+        load_weights(wa, 4, 256, 256)
 
         picked_bytes = keep.tile([P, S], U8, name="picked_bytes", align_bytes=64)
         x_planes = keep.tile([P, PACK, P], U8, name="x_planes", align_bytes=64)
@@ -71,43 +75,83 @@ def tile_picked_bilpool_none_p_kernel(tc, x_words, x_scales, wa, wb, gt, gi, off
         nc.vector.tensor_copy(x_planes[:].rearrange("p t (g r) -> p t g r", r=2), picked_bytes[:].rearrange("p (g t r) -> p t g r", t=PACK, r=2))
         nc.vector.tensor_copy(x_codes[:].rearrange("p t (g r) -> p g t r", r=2), word_table[:].bitcast(U32).indirect(offsets[:]))
 
+        warm_bf = keep.tile([P, 4 * CH], BF16, name="warm_bf", align_bytes=64)
+        warm_codes = keep.tile([P, CH], U32, name="warm_codes", align_bytes=64)
+        warm_planes = keep.tile([P, CH], U8, name="warm_planes", align_bytes=64)
+        nc.vector.memset(warm_bf[:], 0.0)
+        nc.vector.quantize_mx(out=warm_codes[:].bitcast(FP8X4), scales=warm_planes[:], in_=warm_bf[:])
+        warm = psum.tile([P, H], F32, name="pooled0")
+        for k in range(12):
+            nc.tensor.matmul_mx(out=warm[:, (k % 4) * CH : (k % 4 + 1) * CH], lhsT=warm_codes[:, 0:P].bitcast(FP8X4), lhsT_scale=x_planes[:, 0, :], rhs=warm_codes[:].bitcast(FP8X4), rhs_scale=warm_planes[:], start=True, stop=True)
         z2_codes = keep.tile([P, H], U32, name="z2_codes", align_bytes=64)
         z2_planes = keep.tile([P, H], U8, name="z2_planes", align_bytes=64)
 
         w_q = {}
         z_bf = {}
+        w_bf = {}
+        accs = {}
+        w_groups = [[0], [1], [2], [3], [4], [5], [6], [7]]
+        z2_bf = keep.tile([P, H, PACK], BF16, name="z2_bf", align_bytes=64)
+        for grp in w_groups:
+            grouped = keep.tile([P, CH * len(grp), PACK], BF16, name="w_bf%d" % grp[0], align_bytes=64)
+            for k, c in enumerate(grp):
+                w_bf[c] = (grouped, k)
 
-        def cast_w(c):
-            grouped = keep.tile([P, CH, PACK], BF16, name="w_bf%d" % c, align_bytes=64)
-            nc.scalar.copy(grouped[:].rearrange("p (c i) t -> p c t i", i=4), raw_chunks[c].rearrange("p t (c i) -> p c t i", i=4))
-            return grouped
+        def cast_w(c, eng=None):
+            grouped, k = w_bf[c]
+            dst = grouped[:, k * CH : (k + 1) * CH, :].rearrange("p (c i) t -> p c t i", i=4)
+            src = raw_chunks[c].rearrange("p t (c i) -> p c t i", i=4)
+            if eng is None:
+                nc.scalar.copy(dst, src)
+            else:
+                nc.vector.tensor_copy(dst, src)
 
-        def quant_w(c, grouped):
-            codes = keep.tile([P, CH], U32, name="w_codes%d" % c, align_bytes=64)
-            planes = keep.tile([P, CH], U8, name="w_planes%d" % c, align_bytes=64)
-            nc.vector.quantize_mx(out=codes[:].bitcast(FP8X4), scales=planes[:], in_=grouped[:].rearrange("p n t -> p (n t)"))
-            w_q[c] = (codes, planes)
+        def quant_w(c):
+            grp = [g for g in w_groups if g[0] == c][0]
+            codes = keep.tile([P, CH * len(grp)], U32, name="w_codes%d" % c, align_bytes=64)
+            planes = keep.tile([P, CH * len(grp)], U8, name="w_planes%d" % c, align_bytes=64)
+            nc.vector.quantize_mx(out=codes[:].bitcast(FP8X4), scales=planes[:], in_=w_bf[c][0][:].rearrange("p n t -> p (n t)"))
+            for k, d in enumerate(grp):
+                w_q[d] = (codes[:, k * CH : (k + 1) * CH], planes[:, k * CH : (k + 1) * CH])
 
         def project(c):
             codes, planes = w_q[c]
             acc = psum.tile([P, PACK, CH], F32, name="proj%d" % (c % 4))
             for t in range(PACK):
                 nc.tensor.matmul_mx(out=acc[:, t, :], lhsT=x_codes[:, t, :].bitcast(FP8X4), lhsT_scale=x_planes[:, t, :],
-                                    rhs=codes[:].bitcast(FP8X4), rhs_scale=planes[:], start=True, stop=True)
-            return acc
+                                    rhs=codes.bitcast(FP8X4), rhs_scale=planes, start=True, stop=True)
+            accs[c] = acc
 
-        def weigh(c, acc):
-            gate = gi_sb if c < NCH else gt_sb
+        def z_dst(c):
+            if c < NCH:
+                return z2_bf[:, c * CH : (c + 1) * CH, :]
             zb = keep.tile([P, CH, PACK], BF16, name="z_bf%d" % c, align_bytes=64)
-            nc.vector.tensor_tensor(zb[:], acc[:].rearrange("p t n -> p n t"), gate[:, 0:7:2].unsqueeze(1).to_broadcast([P, CH, PACK]), MULT)
             z_bf[c] = zb
+            return zb[:]
+
+        def weigh(c):
+            gate = gi_sb if c < NCH else gt_sb
+            nc.vector.tensor_tensor(z_dst(c), accs[c][:].rearrange("p t n -> p n t"), gate[:, 0:7:2].unsqueeze(1).to_broadcast([P, CH, PACK]), MULT)
+
+        staged = {}
+
+        def weigh_s(c):
+            gate = gi_sb if c < NCH else gt_sb
+            st = keep.tile([P, PACK, CH], BF16, name="staged%d" % c, align_bytes=64)
+            for t in range(PACK):
+                dst = st[:, t, :]
+                nc.scalar.activation(dst, accs[c][:, t, :], COPY, scale=gate[:, 2 * t : 2 * t + 1])
+            staged[c] = st
+
+        def weave(c):
+            nc.vector.tensor_copy(z_dst(c).rearrange("p (c i) t -> p c t i", i=4), staged[c][:].rearrange("p t (c i) -> p c t i", i=4))
+
+        def quant_z2(c0, c1):
+            cols = slice(c0 * CH, c1 * CH)
+            nc.vector.quantize_mx(out=z2_codes[:, cols].bitcast(FP8X4), scales=z2_planes[:, cols], in_=z2_bf[:, cols, :].rearrange("p n t -> p (n t)"))
 
         def quant_z(c):
             src = z_bf[c][:].rearrange("p n t -> p (n t)")
-            if c < NCH:
-                cols = slice(c * CH, (c + 1) * CH)
-                nc.vector.quantize_mx(out=z2_codes[:, cols].bitcast(FP8X4), scales=z2_planes[:, cols], in_=src)
-                return
             i = c - NCH
             codes = keep.tile([P, CH], U32, name="z_codes%d" % i, align_bytes=64)
             planes = keep.tile([P, CH], U8, name="z_planes%d" % i, align_bytes=64)
@@ -134,13 +178,41 @@ def tile_picked_bilpool_none_p_kernel(tc, x_words, x_scales, wa, wb, gt, gi, off
                     nc.vector.tensor_scalar(res[:], pooled[:], 0.0625, None, MULT)
                     nc.sync.dma_start(out[rows, cols], res[:])
 
-        n = 2 * NCH
-        accs = {}
-        for step in range(n + 3):
-            if step < n:
-                quant_w(step, cast_w(step))
-                accs[step] = project(step)
-            if 2 <= step < n + 2:
-                weigh(step - 2, accs[step - 2])
-            if step >= 3:
-                quant_z(step - 3)
+        cast_w(0)
+        quant_w(0)
+        project(0)
+        cast_w(1)
+        quant_w(1)
+        project(1)
+        cast_w(2)
+        quant_w(2)
+        project(2)
+        weigh(0)
+        cast_w(3)
+        quant_w(3)
+        project(3)
+        weigh(1)
+        cast_w(4)
+        quant_w(4)
+        project(4)
+        weigh(2)
+        quant_z2(0, 2)
+        cast_w(5)
+        quant_w(5)
+        project(5)
+        weigh(3)
+        cast_w(6)
+        quant_w(6)
+        project(6)
+        weigh(4)
+        quant_z2(2, 4)
+        cast_w(7)
+        quant_w(7)
+        project(7)
+        weigh(5)
+        quant_z(4)
+        weigh(6)
+        quant_z(5)
+        weigh(7)
+        quant_z(6)
+        quant_z(7)

@@ -17,10 +17,9 @@ COPY = mybir.ActivationFunctionType.Copy
 
 P = 128
 PACK = 4
+RUN = 8
 CH = 128
 NCH = H // CH
-B_LOADS = (128, 128, 128, 128)
-A_LOADS = (256, 256)
 
 
 def tile_picked_bilpool_none_p_kernel(tc, x_words, x_scales, wa, wb, gt, gi, offs, out):
@@ -32,187 +31,183 @@ def tile_picked_bilpool_none_p_kernel(tc, x_words, x_scales, wa, wb, gt, gi, off
         offsets = keep.tile([P, S // 16], U16, name="offsets")
         scale_table = keep.tile([P, T], U8, name="scale_table", align_bytes=64)
         word_table = keep.tile([P, T], I32, name="word_table", align_bytes=64)
-        gi_sb = keep.tile([P, 8], F32, name="gi_sb")
-        gt_sb = keep.tile([P, 8], F32, name="gt_sb")
+        gate_rows = keep.tile([P, P], F32, name="gate_rows", align_bytes=64)
+        gate_dealt = keep.tile([P, P], F32, name="gate_dealt", align_bytes=64)
+        gate_turned = keep.tile([P, P], F32, name="gate_turned", align_bytes=64)
+        gates = keep.tile([P, 2, PACK], F32, name="gates")
 
-        def load_gate(tile, gate):
-            runs = gate.rearrange("(g e) o -> g (e o)", e=8)
-            for r in range(2):
-                nc.sync.dma_start(tile[r:P:2, 0:7], runs[:, r : r + 7])
-
+        def load_gate(row, gate, eng):
+            eng.dma_start(gate_rows[row:P:32, :], gate.rearrange("(q e) o -> q (e o)", q=4))
 
         raw_chunks = {}
 
-        def load_weights(w, first, c0, width):
+        def load_weights(w, first, c0, width, eng=nc.sync):
             raw = keep.tile([P, PACK, width], F32, name="raw%d" % (first + c0 // CH))
-            nc.sync.dma_start(raw[:], w.rearrange("(p t) n -> p t n", t=PACK)[:, :, c0 : c0 + width])
+            eng.dma_start(raw[:], w.rearrange("(p t) n -> p t n", t=PACK)[:, :, c0 : c0 + width])
             for c in range(0, width, CH):
                 raw_chunks[first + (c0 + c) // CH] = raw[:, :, c : c + CH]
 
         def load_scales(q, eng):
             eng.dma_start(scale_table[32 * q : 32 * q + 4, :].bitcast(I32), x_scales[0, 4 * q : 4 * q + 4, :].bitcast(I32))
 
+        def load_words():
+            nc.sync.dma_start(word_table[:], x_words[0].rearrange("p n t -> p (n t)").bitcast(I32))
+
         nc.vector.memset(scale_table[:].bitcast(I32), 0)
+        nc.vector.memset(gate_dealt[:], 0.0)
         nc.sync.dma_start(offsets[:], offs)
-        load_gate(gi_sb, gi)
+        load_gate(0, gt, nc.sync)
+        load_gate(1, gi, nc.sync)
         load_scales(0, nc.sync)
         load_scales(1, nc.sync)
         load_scales(2, nc.scalar)
         load_scales(3, nc.scalar)
-        nc.sync.dma_start(word_table[:], x_words[0].rearrange("p n t -> p (n t)").bitcast(I32))
+        load_words()
         load_weights(wb, 0, 0, 128)
         load_weights(wb, 0, 128, 128)
         load_weights(wb, 0, 256, 128)
         load_weights(wb, 0, 384, 128)
-        load_gate(gt_sb, gt)
         load_weights(wa, 4, 0, 256)
         load_weights(wa, 4, 256, 256)
 
         picked_bytes = keep.tile([P, S], U8, name="picked_bytes", align_bytes=64)
         x_planes = keep.tile([P, PACK, P], U8, name="x_planes", align_bytes=64)
         x_codes = keep.tile([P, PACK, P], U32, name="x_codes", align_bytes=64)
-        nc.vector.tensor_copy(picked_bytes[:], scale_table[:].indirect(offsets[:]))
-        nc.vector.tensor_copy(x_planes[:].rearrange("p t (g r) -> p t g r", r=2), picked_bytes[:].rearrange("p (g t r) -> p t g r", t=PACK, r=2))
-        nc.vector.tensor_copy(x_codes[:].rearrange("p t (g r) -> p g t r", r=2), word_table[:].bitcast(U32).indirect(offsets[:]))
 
-        warm_bf = keep.tile([P, 4 * CH], BF16, name="warm_bf", align_bytes=64)
-        warm_codes = keep.tile([P, CH], U32, name="warm_codes", align_bytes=64)
-        warm_planes = keep.tile([P, CH], U8, name="warm_planes", align_bytes=64)
-        nc.vector.memset(warm_bf[:], 0.0)
-        nc.vector.quantize_mx(out=warm_codes[:].bitcast(FP8X4), scales=warm_planes[:], in_=warm_bf[:])
-        warm = psum.tile([P, H], F32, name="pooled0")
-        for k in range(12):
-            nc.tensor.matmul_mx(out=warm[:, (k % 4) * CH : (k % 4 + 1) * CH], lhsT=warm_codes[:, 0:P].bitcast(FP8X4), lhsT_scale=x_planes[:, 0, :], rhs=warm_codes[:].bitcast(FP8X4), rhs_scale=warm_planes[:], start=True, stop=True)
+        def deal_gates():
+            for q in range(4):
+                rows = slice(32 * q, 32 * q + 2)
+                nc.vector.tensor_copy(gate_dealt[rows, :].rearrange("p (t b r) -> p t b r", t=PACK, r=RUN), gate_rows[rows, :].rearrange("p (b t r) -> p t b r", t=PACK, r=RUN))
+            nc.vector.transpose(gate_turned[:], gate_dealt[:])
+            nc.vector.tensor_copy(gates[:], gate_turned[:].rearrange("p (t i) -> p i t", i=32)[:, 0:2, :])
+
+        def gather_bytes():
+            nc.vector.tensor_copy(picked_bytes[:], scale_table[:].indirect(offsets[:]))
+            nc.vector.tensor_copy(x_planes[:].bitcast(I32).rearrange("p t (b w) -> p t b w", w=2), picked_bytes[:].bitcast(I32).rearrange("p (b t w) -> p t b w", t=PACK, w=2))
+
+        def gather_words():
+            nc.vector.tensor_copy(x_codes[:].rearrange("p t (b r) -> p b t r", r=RUN), word_table[:].bitcast(U32).indirect(offsets[:]))
+
         z2_codes = keep.tile([P, H], U32, name="z2_codes", align_bytes=64)
         z2_planes = keep.tile([P, H], U8, name="z2_planes", align_bytes=64)
-
-        w_q = {}
-        z_bf = {}
-        w_bf = {}
-        accs = {}
-        w_groups = [[0], [1], [2], [3], [4], [5], [6], [7]]
         z2_bf = keep.tile([P, H, PACK], BF16, name="z2_bf", align_bytes=64)
-        for grp in w_groups:
-            grouped = keep.tile([P, CH * len(grp), PACK], BF16, name="w_bf%d" % grp[0], align_bytes=64)
-            for k, c in enumerate(grp):
-                w_bf[c] = (grouped, k)
+        z_codes = keep.tile([P, H], U32, name="z_codes", align_bytes=64)
+        z_planes = keep.tile([P, H], U8, name="z_planes", align_bytes=64)
+        z_bf = keep.tile([P, H, PACK], BF16, name="z_bf", align_bytes=64)
+        w_codes = keep.tile([P, 2 * H], U32, name="w_codes", align_bytes=64)
+        w_planes = keep.tile([P, 2 * H], U8, name="w_planes", align_bytes=64)
+        w_bf = keep.tile([P, 2 * H, PACK], BF16, name="w_bf", align_bytes=64)
+        accs = {}
+        staged = {}
+
+        def cols_of(c0, c1):
+            return slice(c0 * CH, c1 * CH)
 
         def cast_w(c, eng=None):
-            grouped, k = w_bf[c]
-            dst = grouped[:, k * CH : (k + 1) * CH, :].rearrange("p (c i) t -> p c t i", i=4)
+            dst = w_bf[:, cols_of(c, c + 1), :].rearrange("p (c i) t -> p c t i", i=4)
             src = raw_chunks[c].rearrange("p t (c i) -> p c t i", i=4)
             if eng is None:
                 nc.scalar.copy(dst, src)
             else:
                 nc.vector.tensor_copy(dst, src)
 
-        def quant_w(c):
-            grp = [g for g in w_groups if g[0] == c][0]
-            codes = keep.tile([P, CH * len(grp)], U32, name="w_codes%d" % c, align_bytes=64)
-            planes = keep.tile([P, CH * len(grp)], U8, name="w_planes%d" % c, align_bytes=64)
-            nc.vector.quantize_mx(out=codes[:].bitcast(FP8X4), scales=planes[:], in_=w_bf[c][0][:].rearrange("p n t -> p (n t)"))
-            for k, d in enumerate(grp):
-                w_q[d] = (codes[:, k * CH : (k + 1) * CH], planes[:, k * CH : (k + 1) * CH])
+        def quant_w(c0, c1):
+            cols = cols_of(c0, c1)
+            nc.vector.quantize_mx(out=w_codes[:, cols].bitcast(FP8X4), scales=w_planes[:, cols], in_=w_bf[:, cols, :].rearrange("p n t -> p (n t)"))
 
         def project(c):
-            codes, planes = w_q[c]
+            cols = cols_of(c, c + 1)
             acc = psum.tile([P, PACK, CH], F32, name="proj%d" % (c % 4))
             for t in range(PACK):
                 nc.tensor.matmul_mx(out=acc[:, t, :], lhsT=x_codes[:, t, :].bitcast(FP8X4), lhsT_scale=x_planes[:, t, :],
-                                    rhs=codes.bitcast(FP8X4), rhs_scale=planes, start=True, stop=True)
+                                    rhs=w_codes[:, cols].bitcast(FP8X4), rhs_scale=w_planes[:, cols], start=True, stop=True)
             accs[c] = acc
 
         def z_dst(c):
             if c < NCH:
-                return z2_bf[:, c * CH : (c + 1) * CH, :]
-            zb = keep.tile([P, CH, PACK], BF16, name="z_bf%d" % c, align_bytes=64)
-            z_bf[c] = zb
-            return zb[:]
+                return z2_bf[:, cols_of(c, c + 1), :]
+            return z_bf[:, cols_of(c - NCH, c - NCH + 1), :]
 
         def weigh(c):
-            gate = gi_sb if c < NCH else gt_sb
-            nc.vector.tensor_tensor(z_dst(c), accs[c][:].rearrange("p t n -> p n t"), gate[:, 0:7:2].unsqueeze(1).to_broadcast([P, CH, PACK]), MULT)
-
-        staged = {}
+            gate = gates[:, 1 if c < NCH else 0, :]
+            nc.vector.tensor_tensor(z_dst(c), accs[c][:].rearrange("p t n -> p n t"), gate.unsqueeze(1).to_broadcast([P, CH, PACK]), MULT)
 
         def weigh_s(c):
-            gate = gi_sb if c < NCH else gt_sb
             st = keep.tile([P, PACK, CH], BF16, name="staged%d" % c, align_bytes=64)
             for t in range(PACK):
-                dst = st[:, t, :]
-                nc.scalar.activation(dst, accs[c][:, t, :], COPY, scale=gate[:, 2 * t : 2 * t + 1])
+                nc.scalar.activation(st[:, t, :], accs[c][:, t, :], COPY, scale=gates[:, 1 if c < NCH else 0, t : t + 1])
             staged[c] = st
 
         def weave(c):
             nc.vector.tensor_copy(z_dst(c).rearrange("p (c i) t -> p c t i", i=4), staged[c][:].rearrange("p t (c i) -> p c t i", i=4))
 
         def quant_z2(c0, c1):
-            cols = slice(c0 * CH, c1 * CH)
+            cols = cols_of(c0, c1)
             nc.vector.quantize_mx(out=z2_codes[:, cols].bitcast(FP8X4), scales=z2_planes[:, cols], in_=z2_bf[:, cols, :].rearrange("p n t -> p (n t)"))
 
-        def quant_z(c):
-            src = z_bf[c][:].rearrange("p n t -> p (n t)")
-            i = c - NCH
-            codes = keep.tile([P, CH], U32, name="z_codes%d" % i, align_bytes=64)
-            planes = keep.tile([P, CH], U8, name="z_planes%d" % i, align_bytes=64)
-            nc.vector.quantize_mx(out=codes[:].bitcast(FP8X4), scales=planes[:], in_=src)
-            rows = slice(i * CH, (i + 1) * CH)
-            if i < 2:
-                pooled = psum.tile([P, H], F32, name="pooled%d" % i)
-                nc.tensor.matmul_mx(out=pooled[:], lhsT=codes[:].bitcast(FP8X4), lhsT_scale=planes[:],
-                                    rhs=z2_codes[:].bitcast(FP8X4), rhs_scale=z2_planes[:], start=True, stop=True)
-                res = keep.tile([P, H], F32, name="res%d" % i)
-                nc.scalar.activation(res[:], pooled[:], COPY, scale=0.0625)
-                nc.sync.dma_start(out[rows, :], res[:])
-                return
-            for h in range(2):
-                cols = slice(h * 256, (h + 1) * 256)
-                pooled = psum.tile([P, 256], F32, name=("pooled%d" % (2 + h)) if i == 2 else ("proj%d" % h))
-                nc.tensor.matmul_mx(out=pooled[:], lhsT=codes[:].bitcast(FP8X4), lhsT_scale=planes[:],
-                                    rhs=z2_codes[:, cols].bitcast(FP8X4), rhs_scale=z2_planes[:, cols], start=True, stop=True)
-                res = keep.tile([P, 256], F32, name="res%d_%d" % (i, h))
-                if h == 0:
-                    nc.scalar.activation(res[:], pooled[:], COPY, scale=0.0625)
-                    nc.sync.dma_start(out[rows, cols], res[:])
-                else:
-                    nc.vector.tensor_scalar(res[:], pooled[:], 0.0625, None, MULT)
-                    nc.sync.dma_start(out[rows, cols], res[:])
+        def quant_z(i0, i1):
+            cols = cols_of(i0, i1)
+            nc.vector.quantize_mx(out=z_codes[:, cols].bitcast(FP8X4), scales=z_planes[:, cols], in_=z_bf[:, cols, :].rearrange("p n t -> p (n t)"))
 
+        def pool(i, n0, n1, bank, eng, queue=nc.sync):
+            rows = cols_of(i, i + 1)
+            cols = slice(n0, n1)
+            pooled = psum.tile([P, n1 - n0], F32, name=bank)
+            nc.tensor.matmul_mx(out=pooled[:], lhsT=z_codes[:, rows].bitcast(FP8X4), lhsT_scale=z_planes[:, rows],
+                                rhs=z2_codes[:, cols].bitcast(FP8X4), rhs_scale=z2_planes[:, cols], start=True, stop=True)
+            res = keep.tile([P, n1 - n0], F32, name="res%d_%d" % (i, n0))
+            if eng == "s":
+                nc.scalar.activation(res[:], pooled[:], COPY, scale=0.0625)
+            else:
+                nc.vector.tensor_scalar(res[:], pooled[:], 0.0625, None, MULT)
+            queue.dma_start(out[rows, cols], res[:])
+
+        deal_gates()
+        gather_bytes()
+        gather_words()
         cast_w(0)
-        quant_w(0)
+        quant_w(0, 1)
         project(0)
         cast_w(1)
-        quant_w(1)
+        quant_w(1, 2)
         project(1)
         cast_w(2)
-        quant_w(2)
-        project(2)
         weigh(0)
+        quant_w(2, 3)
+        project(2)
         cast_w(3)
-        quant_w(3)
-        project(3)
         weigh(1)
+        quant_w(3, 4)
+        project(3)
         cast_w(4)
-        quant_w(4)
-        project(4)
         weigh(2)
-        quant_z2(0, 2)
+        quant_w(4, 5)
+        project(4)
         cast_w(5)
-        quant_w(5)
+        quant_z2(0, 2)
+        quant_w(5, 6)
         project(5)
-        weigh(3)
         cast_w(6)
-        quant_w(6)
+        weigh(3)
+        quant_w(6, 7)
         project(6)
-        weigh(4)
-        quant_z2(2, 4)
         cast_w(7)
-        quant_w(7)
+        weigh_s(5)
+        weigh(4)
+        quant_w(7, 8)
         project(7)
-        weigh(5)
-        quant_z(4)
-        weigh(6)
-        quant_z(5)
+        weigh_s(6)
+        quant_z2(2, 4)
+        quant_z(0, 1)
+        pool(0, 0, 512, "pooled0", "s")
+        weave(5)
         weigh(7)
-        quant_z(6)
-        quant_z(7)
+        quant_z(1, 2)
+        pool(1, 0, 512, "pooled1", "s")
+        weave(6)
+        quant_z(3, 4)
+        pool(3, 0, 256, "pooled2", "v")
+        pool(3, 256, 512, "pooled3", "v")
+        quant_z(2, 3)
+        pool(2, 0, 256, "proj0", "s")
+        pool(2, 256, 512, "proj1", "v")

@@ -1,6 +1,7 @@
 from contextlib import ExitStack
 
 import concourse.mybir as mybir
+from concourse.masks import make_identity
 
 K, T, S, H = 512, 2048, 512, 512
 FLOPS = 2 * K * S * H * 2 + 2 * S * H * H
@@ -32,12 +33,11 @@ def tile_picked_bilpool_none_p_kernel(tc, x_words, x_scales, wa, wb, gt, gi, off
         scale_table = keep.tile([P, T], U8, name="scale_table", align_bytes=64)
         word_table = keep.tile([P, T], I32, name="word_table", align_bytes=64)
         gate_rows = keep.tile([P, P], F32, name="gate_rows", align_bytes=64)
-        gate_dealt = keep.tile([P, P], F32, name="gate_dealt", align_bytes=64)
-        gate_turned = keep.tile([P, P], F32, name="gate_turned", align_bytes=64)
+        ident = keep.tile([P, P], F32, name="ident", align_bytes=64)
         gates = keep.tile([P, 2, PACK], F32, name="gates")
 
         def load_gate(row, gate, eng):
-            eng.dma_start(gate_rows[row:P:32, :], gate.rearrange("(q e) o -> q (e o)", q=4))
+            eng.dma_start(gate_rows[PACK * row : PACK * (row + 1), :].rearrange("t (b r) -> t b r", r=RUN), gate.rearrange("(b t r) o -> t b (r o)", t=PACK, r=RUN))
 
         raw_chunks = {}
 
@@ -50,36 +50,39 @@ def tile_picked_bilpool_none_p_kernel(tc, x_words, x_scales, wa, wb, gt, gi, off
         def load_scales(q, eng):
             eng.dma_start(scale_table[32 * q : 32 * q + 4, :].bitcast(I32), x_scales[0, 4 * q : 4 * q + 4, :].bitcast(I32))
 
-        def load_words():
-            nc.sync.dma_start(word_table[:], x_words[0].rearrange("p n t -> p (n t)").bitcast(I32))
+        def load_words(c0, c1):
+            nc.sync.dma_start(word_table[:, c0:c1], x_words[0].rearrange("p n t -> p (n t)").bitcast(I32)[:, c0:c1])
 
         nc.vector.memset(scale_table[:].bitcast(I32), 0)
-        nc.vector.memset(gate_dealt[:], 0.0)
+        nc.vector.memset(gate_rows[:], 0.0)
+        nc.vector.memset(ident[:], 0.0)
+        make_identity(nc, ident[:], nomemset=True)
         nc.sync.dma_start(offsets[:], offs)
-        load_gate(0, gt, nc.sync)
-        load_gate(1, gi, nc.sync)
+        load_words(0, 512)
         load_scales(0, nc.sync)
         load_scales(1, nc.sync)
         load_scales(2, nc.scalar)
         load_scales(3, nc.scalar)
-        load_words()
+        load_words(512, 2048)
+        load_gate(1, gi, nc.sync)
+        load_gate(0, gt, nc.sync)
         load_weights(wb, 0, 0, 128)
         load_weights(wb, 0, 128, 128)
+        load_weights(wa, 4, 0, 128)
+        load_weights(wa, 4, 128, 128)
         load_weights(wb, 0, 256, 128)
         load_weights(wb, 0, 384, 128)
-        load_weights(wa, 4, 0, 256)
-        load_weights(wa, 4, 256, 256)
+        load_weights(wa, 4, 256, 128)
+        load_weights(wa, 4, 384, 128)
 
         picked_bytes = keep.tile([P, S], U8, name="picked_bytes", align_bytes=64)
         x_planes = keep.tile([P, PACK, P], U8, name="x_planes", align_bytes=64)
         x_codes = keep.tile([P, PACK, P], U32, name="x_codes", align_bytes=64)
 
         def deal_gates():
-            for q in range(4):
-                rows = slice(32 * q, 32 * q + 2)
-                nc.vector.tensor_copy(gate_dealt[rows, :].rearrange("p (t b r) -> p t b r", t=PACK, r=RUN), gate_rows[rows, :].rearrange("p (b t r) -> p t b r", t=PACK, r=RUN))
-            nc.vector.transpose(gate_turned[:], gate_dealt[:])
-            nc.vector.tensor_copy(gates[:], gate_turned[:].rearrange("p (t i) -> p i t", i=32)[:, 0:2, :])
+            turned = psum.tile([P, P], F32, name="pooled3")
+            nc.tensor.transpose(turned[:], gate_rows[:], ident[:])
+            nc.vector.tensor_copy(gates[:].rearrange("p i t -> p (i t)"), turned[:, 0 : 2 * PACK])
 
         def gather_bytes():
             nc.vector.tensor_copy(picked_bytes[:], scale_table[:].indirect(offsets[:]))
@@ -115,9 +118,9 @@ def tile_picked_bilpool_none_p_kernel(tc, x_words, x_scales, wa, wb, gt, gi, off
             cols = cols_of(c0, c1)
             nc.vector.quantize_mx(out=w_codes[:, cols].bitcast(FP8X4), scales=w_planes[:, cols], in_=w_bf[:, cols, :].rearrange("p n t -> p (n t)"))
 
-        def project(c):
+        def project(c, bank):
             cols = cols_of(c, c + 1)
-            acc = psum.tile([P, PACK, CH], F32, name="proj%d" % (c % 4))
+            acc = psum.tile([P, PACK, CH], F32, name="proj%d" % bank)
             for t in range(PACK):
                 nc.tensor.matmul_mx(out=acc[:, t, :], lhsT=x_codes[:, t, :].bitcast(FP8X4), lhsT_scale=x_planes[:, t, :],
                                     rhs=w_codes[:, cols].bitcast(FP8X4), rhs_scale=w_planes[:, cols], start=True, stop=True)
@@ -161,53 +164,62 @@ def tile_picked_bilpool_none_p_kernel(tc, x_words, x_scales, wa, wb, gt, gi, off
             else:
                 nc.vector.tensor_scalar(res[:], pooled[:], 0.0625, None, MULT)
             queue.dma_start(out[rows, cols], res[:])
+            return res
 
-        deal_gates()
+        def pool_pair(n0, bank):
+            cols = slice(n0, n0 + 256)
+            pooled = psum.tile([P, 2, 256], F32, name=bank)
+            for i in range(2):
+                rows = cols_of(i, i + 1)
+                nc.tensor.matmul_mx(out=pooled[:, i, :], lhsT=z_codes[:, rows].bitcast(FP8X4), lhsT_scale=z_planes[:, rows],
+                                    rhs=z2_codes[:, cols].bitcast(FP8X4), rhs_scale=z2_planes[:, cols], start=True, stop=True)
+            res = keep.tile([P, 2, 256], F32, name="pair%d" % n0)
+            nc.scalar.activation(res[:], pooled[:], COPY, scale=0.0625)
+            nc.sync.dma_start(out[0:256, cols].rearrange("(i p) n -> p i n", i=2), res[:])
+            return res
+
         gather_bytes()
         gather_words()
         cast_w(0)
         quant_w(0, 1)
-        project(0)
+        project(0, 0)
+        deal_gates()
         cast_w(1)
         quant_w(1, 2)
-        project(1)
-        cast_w(2)
-        weigh(0)
-        quant_w(2, 3)
-        project(2)
-        cast_w(3)
-        weigh(1)
-        quant_w(3, 4)
-        project(3)
+        project(1, 1)
         cast_w(4)
-        weigh(2)
+        weigh(0)
         quant_w(4, 5)
-        project(4)
+        project(4, 2)
         cast_w(5)
-        quant_z2(0, 2)
+        weigh(1)
         quant_w(5, 6)
-        project(5)
-        cast_w(6)
-        weigh(3)
-        quant_w(6, 7)
-        project(6)
-        cast_w(7)
-        weigh_s(5)
+        project(5, 3)
+        cast_w(2)
         weigh(4)
-        quant_w(7, 8)
-        project(7)
-        weigh_s(6)
+        quant_w(2, 3)
+        project(2, 0)
+        cast_w(3)
+        quant_z2(0, 2)
+        quant_w(3, 4)
+        project(3, 1)
+        cast_w(6)
+        cast_w(7)
+        weigh(5)
+        weigh_s(3)
+        quant_w(6, 8)
+        project(6, 2)
+        project(7, 3)
+        quant_z(0, 2)
+        pool_pair(0, "pooled0")
+        weigh(2)
+        weave(3)
+        weigh(6)
         quant_z2(2, 4)
-        quant_z(0, 1)
-        pool(0, 0, 512, "pooled0", "s")
-        weave(5)
-        weigh(7)
-        quant_z(1, 2)
-        pool(1, 0, 512, "pooled1", "s")
-        weave(6)
-        quant_z(3, 4)
-        pool(3, 0, 256, "pooled2", "v")
-        pool(3, 256, 512, "pooled3", "v")
+        pool_pair(256, "pooled1")
         quant_z(2, 3)
-        pool(2, 0, 256, "proj0", "s")
-        pool(2, 256, 512, "proj1", "v")
+        pool(2, 0, 512, "pooled2", "s")
+        weigh(7)
+        quant_z(3, 4)
+        pool(3, 0, 256, "pooled3", "s")
+        pool(3, 256, 512, "proj0", "v")

@@ -61,8 +61,8 @@ def tile_picked_bilpool_none_p_kernel(tc, x_words, x_scales, wa, wb, gt, gi, off
         load_words(0, 512)
         load_scales(0, nc.sync)
         load_scales(1, nc.sync)
-        load_scales(2, nc.scalar)
-        load_scales(3, nc.scalar)
+        load_scales(2, nc.sync)
+        load_scales(3, nc.sync)
         load_words(512, 2048)
         load_gate(1, gi, nc.sync)
         load_gate(0, gt, nc.sync)

@@ -1,7 +1,6 @@
 from contextlib import ExitStack
 
 import concourse.mybir as mybir
-from concourse.masks import make_identity
 
 K, T, S, H = 512, 2048, 512, 512
 FLOPS = 2 * K * S * H * 2 + 2 * S * H * H
@@ -17,10 +16,21 @@ MULT = mybir.AluOpType.mult
 COPY = mybir.ActivationFunctionType.Copy
 
 P = 128
-PACK = 4
+QUAD = 32
+QUADS = P // QUAD
+SLOTS = 4
 RUN = 8
 CH = 128
-NCH = H // CH
+HALF = H // 2
+WALK = 4
+EARLY_WORDS = T // 4
+POOL_SCALE = 0.0625
+
+B, A = 0, 1
+B0, B1, B2, B3 = [(B, i) for i in range(4)]
+A0, A1, A2, A3 = [(A, i) for i in range(4)]
+ORDER = (B0, B1, A0, A1, B2, B3, A2, A3)
+PROJ_BANKS = 4
 
 
 def tile_picked_bilpool_none_p_kernel(tc, x_words, x_scales, wa, wb, gt, gi, offs, out):
@@ -29,197 +39,160 @@ def tile_picked_bilpool_none_p_kernel(tc, x_words, x_scales, wa, wb, gt, gi, off
         keep = ctx.enter_context(tc.tile_pool(name="keep", bufs=1))
         psum = ctx.enter_context(tc.psum_pool(name="psum", bufs=1))
 
+        def columns(first, last):
+            return slice(first * CH, last * CH)
+
+        def tag(name, chunk):
+            return "%s_%d_%d" % (name, chunk[0], chunk[1])
+
         offsets = keep.tile([P, S // 16], U16, name="offsets")
         scale_table = keep.tile([P, T], U8, name="scale_table", align_bytes=64)
         word_table = keep.tile([P, T], I32, name="word_table", align_bytes=64)
         gate_rows = keep.tile([P, P], F32, name="gate_rows", align_bytes=64)
-        ident = keep.tile([P, P], F32, name="ident", align_bytes=64)
-        gates = keep.tile([P, 2, PACK], F32, name="gates")
+        w_raw = {}
 
-        def load_gate(row, gate, eng):
-            eng.dma_start(gate_rows[PACK * row : PACK * (row + 1), :].rearrange("t (b r) -> t b r", r=RUN), gate.rearrange("(b t r) o -> t b (r o)", t=PACK, r=RUN))
+        def load_words(cols):
+            nc.sync.dma_start(word_table[:, cols], x_words[0].rearrange("p n t -> p (n t)").bitcast(I32)[:, cols])
 
-        raw_chunks = {}
-
-        def load_weights(w, first, c0, width, eng=nc.sync):
-            raw = keep.tile([P, PACK, width], F32, name="raw%d" % (first + c0 // CH))
-            eng.dma_start(raw[:], w.rearrange("(p t) n -> p t n", t=PACK)[:, :, c0 : c0 + width])
-            for c in range(0, width, CH):
-                raw_chunks[first + (c0 + c) // CH] = raw[:, :, c : c + CH]
-
-        def load_scales(q, eng):
-            eng.dma_start(scale_table[32 * q : 32 * q + 4, :].bitcast(I32), x_scales[0, 4 * q : 4 * q + 4, :].bitcast(I32))
-
-        def load_words(c0, c1):
-            nc.sync.dma_start(word_table[:, c0:c1], x_words[0].rearrange("p n t -> p (n t)").bitcast(I32)[:, c0:c1])
+        def load_weights(chunk):
+            side, i = chunk
+            raw = keep.tile([P, SLOTS, CH], F32, name=tag("w_raw", chunk))
+            nc.sync.dma_start(raw[:], (wb, wa)[side].rearrange("(p t) n -> p t n", t=SLOTS)[:, :, columns(i, i + 1)])
+            w_raw[chunk] = raw
 
         nc.vector.memset(scale_table[:].bitcast(I32), 0)
         nc.vector.memset(gate_rows[:], 0.0)
-        nc.vector.memset(ident[:], 0.0)
-        make_identity(nc, ident[:], nomemset=True)
         nc.sync.dma_start(offsets[:], offs)
-        load_words(0, 512)
-        load_scales(0, nc.sync)
-        load_scales(1, nc.sync)
-        load_scales(2, nc.sync)
-        load_scales(3, nc.sync)
-        load_words(512, 2048)
-        load_gate(1, gi, nc.sync)
-        load_gate(0, gt, nc.sync)
-        load_weights(wb, 0, 0, 128)
-        load_weights(wb, 0, 128, 128)
-        load_weights(wa, 4, 0, 128)
-        load_weights(wa, 4, 128, 128)
-        load_weights(wb, 0, 256, 128)
-        load_weights(wb, 0, 384, 128)
-        load_weights(wa, 4, 256, 128)
-        load_weights(wa, 4, 384, 128)
+        load_words(slice(0, EARLY_WORDS))
+        for q in range(QUADS):
+            nc.sync.dma_start(scale_table[QUAD * q : QUAD * q + 4, :].bitcast(I32), x_scales[0, 4 * q : 4 * q + 4, :].bitcast(I32))
+        load_words(slice(EARLY_WORDS, T))
+        load_weights(B0)
+        load_weights(B1)
+        for side, gate in ((B, gi), (A, gt)):
+            nc.sync.dma_start(gate_rows[side:P:QUAD, :], gate.rearrange("(q e) o -> q (e o)", q=QUADS))
+        for chunk in ORDER[2:]:
+            load_weights(chunk)
 
         picked_bytes = keep.tile([P, S], U8, name="picked_bytes", align_bytes=64)
-        x_planes = keep.tile([P, PACK, P], U8, name="x_planes", align_bytes=64)
-        x_codes = keep.tile([P, PACK, P], U32, name="x_codes", align_bytes=64)
+        x_planes = keep.tile([P, SLOTS, P], U8, name="x_planes", align_bytes=64)
+        x_codes = keep.tile([P, SLOTS, P], U32, name="x_codes", align_bytes=64)
+        nc.vector.tensor_copy(picked_bytes[:], scale_table[:].indirect(offsets[:]))
+        nc.vector.tensor_copy(
+            x_planes[:].bitcast(I32).rearrange("p t (j w) -> p t j w", w=RUN // 4),
+            picked_bytes[:].bitcast(I32).rearrange("p (j t w) -> p t j w", t=SLOTS, w=RUN // 4),
+        )
+        nc.vector.tensor_copy(x_codes[:].rearrange("p t (j r) -> p j t r", r=RUN), word_table[:].bitcast(U32).indirect(offsets[:]))
+
+        gates = keep.tile([P, 2, SLOTS], F32, name="gates")
+        z_bf = [keep.tile([P, H, SLOTS], BF16, name="z_bf%d" % side, align_bytes=64) for side in (B, A)]
+        z_codes = [keep.tile([P, H], U32, name="z_codes%d" % side, align_bytes=64) for side in (B, A)]
+        z_planes = [keep.tile([P, H], U8, name="z_planes%d" % side, align_bytes=64) for side in (B, A)]
+        w_bf = {}
+        projected = {}
+        weighed = {}
 
         def deal_gates():
-            turned = psum.tile([P, P], F32, name="pooled3")
-            nc.tensor.transpose(turned[:], gate_rows[:], ident[:])
-            nc.vector.tensor_copy(gates[:].rearrange("p i t -> p (i t)"), turned[:, 0 : 2 * PACK])
+            dealt = keep.tile([P, P], F32, name=tag("w_bf", B0), align_bytes=64)
+            turned = keep.tile([P, P], F32, name="gate_turned", align_bytes=64)
+            nc.vector.tensor_copy(dealt[:].rearrange("p (t j r) -> p t j r", t=SLOTS, r=RUN), gate_rows[:].rearrange("p (j t r) -> p t j r", t=SLOTS, r=RUN))
+            nc.vector.transpose(turned[:], dealt[:])
+            nc.vector.tensor_copy(gates[:], turned[:].rearrange("p (t i) -> p i t", i=QUAD)[:, 0:2, :])
 
-        def gather_bytes():
-            nc.vector.tensor_copy(picked_bytes[:], scale_table[:].indirect(offsets[:]))
-            nc.vector.tensor_copy(x_planes[:].bitcast(I32).rearrange("p t (b w) -> p t b w", w=2), picked_bytes[:].bitcast(I32).rearrange("p (b t w) -> p t b w", t=PACK, w=2))
+        def interleave(copy, words, slots):
+            copy(words.rearrange("p (c i) t -> p c t i", i=WALK), slots.rearrange("p t (c i) -> p c t i", i=WALK))
 
-        def gather_words():
-            nc.vector.tensor_copy(x_codes[:].rearrange("p t (b r) -> p b t r", r=RUN), word_table[:].bitcast(U32).indirect(offsets[:]))
+        def round_weights(chunk):
+            w_bf[chunk] = keep.tile([P, CH, SLOTS], BF16, name=tag("w_bf", chunk), align_bytes=64)
+            interleave(nc.scalar.copy, w_bf[chunk][:], w_raw[chunk][:])
 
-        z2_codes = keep.tile([P, H], U32, name="z2_codes", align_bytes=64)
-        z2_planes = keep.tile([P, H], U8, name="z2_planes", align_bytes=64)
-        z2_bf = keep.tile([P, H, PACK], BF16, name="z2_bf", align_bytes=64)
-        z_codes = keep.tile([P, H], U32, name="z_codes", align_bytes=64)
-        z_planes = keep.tile([P, H], U8, name="z_planes", align_bytes=64)
-        z_bf = keep.tile([P, H, PACK], BF16, name="z_bf", align_bytes=64)
-        w_codes = keep.tile([P, 2 * H], U32, name="w_codes", align_bytes=64)
-        w_planes = keep.tile([P, 2 * H], U8, name="w_planes", align_bytes=64)
-        w_bf = keep.tile([P, 2 * H, PACK], BF16, name="w_bf", align_bytes=64)
-        accs = {}
-        staged = {}
-
-        def cols_of(c0, c1):
-            return slice(c0 * CH, c1 * CH)
-
-        def cast_w(c, eng=None):
-            dst = w_bf[:, cols_of(c, c + 1), :].rearrange("p (c i) t -> p c t i", i=4)
-            src = raw_chunks[c].rearrange("p t (c i) -> p c t i", i=4)
-            if eng is None:
-                nc.scalar.copy(dst, src)
-            else:
-                nc.vector.tensor_copy(dst, src)
-
-        def quant_w(c0, c1):
-            cols = cols_of(c0, c1)
-            nc.vector.quantize_mx(out=w_codes[:, cols].bitcast(FP8X4), scales=w_planes[:, cols], in_=w_bf[:, cols, :].rearrange("p n t -> p (n t)"))
-
-        def project(c, bank):
-            cols = cols_of(c, c + 1)
-            acc = psum.tile([P, PACK, CH], F32, name="proj%d" % bank)
-            for t in range(PACK):
+        def project(chunk):
+            codes = keep.tile([P, CH], U32, name=tag("w_codes", chunk), align_bytes=64)
+            planes = keep.tile([P, CH], U8, name=tag("w_planes", chunk), align_bytes=64)
+            nc.vector.quantize_mx(out=codes[:].bitcast(FP8X4), scales=planes[:], in_=w_bf[chunk][:].rearrange("p n t -> p (n t)"))
+            acc = psum.tile([P, SLOTS, CH], F32, name="proj%d" % (ORDER.index(chunk) % PROJ_BANKS))
+            for t in range(SLOTS):
                 nc.tensor.matmul_mx(out=acc[:, t, :], lhsT=x_codes[:, t, :].bitcast(FP8X4), lhsT_scale=x_planes[:, t, :],
-                                    rhs=w_codes[:, cols].bitcast(FP8X4), rhs_scale=w_planes[:, cols], start=True, stop=True)
-            accs[c] = acc
+                                    rhs=codes[:].bitcast(FP8X4), rhs_scale=planes[:], start=True, stop=True)
+            projected[chunk] = acc
 
-        def z_dst(c):
-            if c < NCH:
-                return z2_bf[:, cols_of(c, c + 1), :]
-            return z_bf[:, cols_of(c - NCH, c - NCH + 1), :]
+        def weigh_on_vector(chunk):
+            side, i = chunk
+            nc.vector.tensor_tensor(z_bf[side][:, columns(i, i + 1), :], projected[chunk][:].rearrange("p t n -> p n t"),
+                                    gates[:, side, :].unsqueeze(1).to_broadcast([P, CH, SLOTS]), MULT)
 
-        def weigh(c):
-            gate = gates[:, 1 if c < NCH else 0, :]
-            nc.vector.tensor_tensor(z_dst(c), accs[c][:].rearrange("p t n -> p n t"), gate.unsqueeze(1).to_broadcast([P, CH, PACK]), MULT)
+        def weigh_on_scalar(chunk):
+            weighed[chunk] = keep.tile([P, SLOTS, CH], BF16, name=tag("weighed", chunk), align_bytes=64)
+            for t in range(SLOTS):
+                nc.scalar.activation(weighed[chunk][:, t, :], projected[chunk][:, t, :], COPY, scale=gates[:, chunk[0], t : t + 1])
 
-        def weigh_s(c):
-            st = keep.tile([P, PACK, CH], BF16, name="staged%d" % c, align_bytes=64)
-            for t in range(PACK):
-                nc.scalar.activation(st[:, t, :], accs[c][:, t, :], COPY, scale=gates[:, 1 if c < NCH else 0, t : t + 1])
-            staged[c] = st
+        def interleave_weighed(chunk):
+            side, i = chunk
+            interleave(nc.vector.tensor_copy, z_bf[side][:, columns(i, i + 1), :], weighed[chunk][:])
 
-        def weave(c):
-            nc.vector.tensor_copy(z_dst(c).rearrange("p (c i) t -> p c t i", i=4), staged[c][:].rearrange("p t (c i) -> p c t i", i=4))
+        def quantise_z(first, last):
+            side, cols = first[0], columns(first[1], last[1] + 1)
+            nc.vector.quantize_mx(out=z_codes[side][:, cols].bitcast(FP8X4), scales=z_planes[side][:, cols],
+                                  in_=z_bf[side][:, cols, :].rearrange("p n t -> p (n t)"))
 
-        def quant_z2(c0, c1):
-            cols = cols_of(c0, c1)
-            nc.vector.quantize_mx(out=z2_codes[:, cols].bitcast(FP8X4), scales=z2_planes[:, cols], in_=z2_bf[:, cols, :].rearrange("p n t -> p (n t)"))
+        def pool_pass(acc, i, half):
+            rows, cols = columns(i, i + 1), slice(half * HALF, (half + 1) * HALF)
+            nc.tensor.matmul_mx(out=acc, lhsT=z_codes[A][:, rows].bitcast(FP8X4), lhsT_scale=z_planes[A][:, rows],
+                                rhs=z_codes[B][:, cols].bitcast(FP8X4), rhs_scale=z_planes[B][:, cols], start=True, stop=True)
 
-        def quant_z(i0, i1):
-            cols = cols_of(i0, i1)
-            nc.vector.quantize_mx(out=z_codes[:, cols].bitcast(FP8X4), scales=z_planes[:, cols], in_=z_bf[:, cols, :].rearrange("p n t -> p (n t)"))
-
-        def pool(i, n0, n1, bank, eng, queue=nc.sync):
-            rows = cols_of(i, i + 1)
-            cols = slice(n0, n1)
-            pooled = psum.tile([P, n1 - n0], F32, name=bank)
-            nc.tensor.matmul_mx(out=pooled[:], lhsT=z_codes[:, rows].bitcast(FP8X4), lhsT_scale=z_planes[:, rows],
-                                rhs=z2_codes[:, cols].bitcast(FP8X4), rhs_scale=z2_planes[:, cols], start=True, stop=True)
-            res = keep.tile([P, n1 - n0], F32, name="res%d_%d" % (i, n0))
-            if eng == "s":
-                nc.scalar.activation(res[:], pooled[:], COPY, scale=0.0625)
-            else:
-                nc.vector.tensor_scalar(res[:], pooled[:], 0.0625, None, MULT)
-            queue.dma_start(out[rows, cols], res[:])
-            return res
-
-        def pool_pair(n0, bank):
-            cols = slice(n0, n0 + 256)
-            pooled = psum.tile([P, 2, 256], F32, name=bank)
+        def pool_first_quarter(bank):
+            acc = psum.tile([P, 2, HALF], F32, name=bank)
             for i in range(2):
-                rows = cols_of(i, i + 1)
-                nc.tensor.matmul_mx(out=pooled[:, i, :], lhsT=z_codes[:, rows].bitcast(FP8X4), lhsT_scale=z_planes[:, rows],
-                                    rhs=z2_codes[:, cols].bitcast(FP8X4), rhs_scale=z2_planes[:, cols], start=True, stop=True)
-            res = keep.tile([P, 2, 256], F32, name="pair%d" % n0)
-            nc.scalar.activation(res[:], pooled[:], COPY, scale=0.0625)
-            nc.sync.dma_start(out[0:256, cols].rearrange("(i p) n -> p i n", i=2), res[:])
-            return res
+                pool_pass(acc[:, i, :], i, 0)
+            res = keep.tile([P, 2, HALF], F32, name="res_quarter")
+            nc.scalar.activation(res[:], acc[:], COPY, scale=POOL_SCALE)
+            nc.sync.dma_start(out[0:HALF, 0:HALF].rearrange("(i p) n -> p i n", i=2), res[:])
 
-        gather_bytes()
-        gather_words()
-        cast_w(0)
-        quant_w(0, 1)
-        project(0, 0)
+        def pool_piece(i, half, bank, on_scalar):
+            acc = psum.tile([P, HALF], F32, name=bank)
+            pool_pass(acc[:], i, half)
+            res = keep.tile([P, HALF], F32, name="res%d_%d" % (i, half))
+            if on_scalar:
+                nc.scalar.activation(res[:], acc[:], COPY, scale=POOL_SCALE)
+            else:
+                nc.vector.tensor_scalar(res[:], acc[:], POOL_SCALE, None, MULT)
+            nc.sync.dma_start(out[columns(i, i + 1), half * HALF : (half + 1) * HALF], res[:])
+
+        round_weights(B0)
+        project(B0)
         deal_gates()
-        cast_w(1)
-        quant_w(1, 2)
-        project(1, 1)
-        cast_w(4)
-        weigh(0)
-        quant_w(4, 5)
-        project(4, 2)
-        cast_w(5)
-        weigh(1)
-        quant_w(5, 6)
-        project(5, 3)
-        cast_w(2)
-        weigh(4)
-        quant_w(2, 3)
-        project(2, 0)
-        cast_w(3)
-        quant_z2(0, 2)
-        quant_w(3, 4)
-        project(3, 1)
-        cast_w(6)
-        cast_w(7)
-        weigh(5)
-        weigh_s(3)
-        quant_w(6, 8)
-        project(6, 2)
-        project(7, 3)
-        quant_z(0, 2)
-        pool_pair(0, "pooled0")
-        weigh(2)
-        weave(3)
-        weigh(6)
-        quant_z2(2, 4)
-        pool_pair(256, "pooled1")
-        quant_z(2, 3)
-        pool(2, 0, 512, "pooled2", "s")
-        weigh(7)
-        quant_z(3, 4)
-        pool(3, 0, 256, "pooled3", "s")
-        pool(3, 256, 512, "proj0", "v")
+        for chunk in (B1, A0):
+            round_weights(chunk)
+            project(chunk)
+        round_weights(A1)
+        weigh_on_vector(B0)
+        project(A1)
+        round_weights(B2)
+        weigh_on_vector(B1)
+        project(B2)
+        round_weights(B3)
+        weigh_on_scalar(A1)
+        weigh_on_vector(A0)
+        project(B3)
+        round_weights(A2)
+        quantise_z(B0, B1)
+        interleave_weighed(A1)
+        round_weights(A3)
+        weigh_on_scalar(B3)
+        weigh_on_vector(B2)
+        project(A2)
+        quantise_z(A0, A1)
+        pool_first_quarter("pool0")
+        project(A3)
+        weigh_on_vector(A2)
+        interleave_weighed(B3)
+        quantise_z(A2, A2)
+        quantise_z(B2, B3)
+        pool_piece(0, 1, "pool1", True)
+        pool_piece(2, 0, "pool3", True)
+        weigh_on_vector(A3)
+        pool_piece(1, 1, "pool2", False)
+        quantise_z(A3, A3)
+        pool_piece(2, 1, "proj0", False)
+        pool_piece(3, 0, "proj1", True)
+        pool_piece(3, 1, "pool0", False)

@@ -23,7 +23,7 @@ RUN = 8
 CH = 128
 HALF = H // 2
 WALK = 4
-EARLY_WORDS = T // 4
+EARLY_WORDS = 3 * T // 8
 POOL_SCALE = 0.0625
 
 B, A = 0, 1
@@ -56,11 +56,12 @@ def tile_picked_bilpool_none_p_kernel(tc, x_words, x_scales, wa, wb, gt, gi, off
 
         def load_weights(chunk):
             side, i = chunk
-            raw = keep.tile([P, SLOTS, CH], F32, name=tag("w_raw", chunk))
+            raw = keep.tile([P, SLOTS, CH], F32, name=tag("w_raw", chunk), align_bytes=64)
             nc.sync.dma_start(raw[:], (wb, wa)[side].rearrange("(p t) n -> p t n", t=SLOTS)[:, :, columns(i, i + 1)])
             w_raw[chunk] = raw
 
-        nc.vector.memset(scale_table[:].bitcast(I32), 0)
+        nc.vector.memset(scale_table[:, 0 : T // 2].bitcast(I32), 0)
+        nc.gpsimd.memset(scale_table[:, T // 2 : T].bitcast(I32), 0)
         nc.vector.memset(gate_rows[:], 0.0)
         nc.sync.dma_start(offsets[:], offs)
         load_words(slice(0, EARLY_WORDS))
@@ -75,13 +76,8 @@ def tile_picked_bilpool_none_p_kernel(tc, x_words, x_scales, wa, wb, gt, gi, off
             load_weights(chunk)
 
         picked_bytes = keep.tile([P, S], U8, name="picked_bytes", align_bytes=64)
-        x_planes = keep.tile([P, SLOTS, P], U8, name="x_planes", align_bytes=64)
         x_codes = keep.tile([P, SLOTS, P], U32, name="x_codes", align_bytes=64)
         nc.vector.tensor_copy(picked_bytes[:], scale_table[:].indirect(offsets[:]))
-        nc.vector.tensor_copy(
-            x_planes[:].bitcast(I32).rearrange("p t (j w) -> p t j w", w=RUN // 4),
-            picked_bytes[:].bitcast(I32).rearrange("p (j t w) -> p t j w", t=SLOTS, w=RUN // 4),
-        )
         nc.vector.tensor_copy(x_codes[:].rearrange("p t (j r) -> p j t r", r=RUN), word_table[:].bitcast(U32).indirect(offsets[:]))
 
         gates = keep.tile([P, 2, SLOTS], F32, name="gates")
@@ -159,6 +155,11 @@ def tile_picked_bilpool_none_p_kernel(tc, x_words, x_scales, wa, wb, gt, gi, off
             nc.sync.dma_start(out[columns(i, i + 1), half * HALF : (half + 1) * HALF], res[:])
 
         round_weights(B0)
+        x_planes = keep.tile([P, SLOTS, P], U8, name=tag("w_raw", B0), align_bytes=64)
+        nc.vector.tensor_copy(
+            x_planes[:].bitcast(I32).rearrange("p t (j w) -> p t j w", w=RUN // 4),
+            picked_bytes[:].bitcast(I32).rearrange("p (j t w) -> p t j w", t=SLOTS, w=RUN // 4),
+        )
         project(B0)
         deal_gates()
         for chunk in (B1, A0):
@@ -177,17 +178,18 @@ def tile_picked_bilpool_none_p_kernel(tc, x_words, x_scales, wa, wb, gt, gi, off
         round_weights(A2)
         quantise_z(B0, B1)
         interleave_weighed(A1)
+        project(A2)
         round_weights(A3)
         weigh_on_scalar(B3)
+        weigh_on_scalar(A2)
         weigh_on_vector(B2)
-        project(A2)
+        project(A3)
         quantise_z(A0, A1)
         pool_first_quarter("pool0")
-        project(A3)
-        weigh_on_vector(A2)
         interleave_weighed(B3)
-        quantise_z(A2, A2)
+        interleave_weighed(A2)
         quantise_z(B2, B3)
+        quantise_z(A2, A2)
         pool_piece(0, 1, "pool1", True)
         pool_piece(2, 0, "pool3", True)
         weigh_on_vector(A3)

@@ -63,8 +63,8 @@ def tile_picked_bilpool_none_p_kernel(tc, x_words, x_scales, wa, wb, gt, gi, off
         nc.vector.memset(scale_table[:, 0 : T // 2].bitcast(I32), 0)
         nc.gpsimd.memset(scale_table[:, T // 2 : T].bitcast(I32), 0)
         nc.vector.memset(gate_rows[:], 0.0)
-        nc.sync.dma_start(offsets[:], offs)
         load_words(slice(0, EARLY_WORDS))
+        nc.sync.dma_start(offsets[:], offs)
         for q in range(QUADS):
             nc.sync.dma_start(scale_table[QUAD * q : QUAD * q + 4, :].bitcast(I32), x_scales[0, 4 * q : 4 * q + 4, :].bitcast(I32))
         load_words(slice(EARLY_WORDS, T))
@@ -178,18 +178,17 @@ def tile_picked_bilpool_none_p_kernel(tc, x_words, x_scales, wa, wb, gt, gi, off
         round_weights(A2)
         quantise_z(B0, B1)
         interleave_weighed(A1)
-        project(A2)
         round_weights(A3)
         weigh_on_scalar(B3)
-        weigh_on_scalar(A2)
         weigh_on_vector(B2)
-        project(A3)
+        project(A2)
         quantise_z(A0, A1)
         pool_first_quarter("pool0")
+        project(A3)
+        weigh_on_vector(A2)
         interleave_weighed(B3)
-        interleave_weighed(A2)
-        quantise_z(B2, B3)
         quantise_z(A2, A2)
+        quantise_z(B2, B3)
         pool_piece(0, 1, "pool1", True)
         pool_piece(2, 0, "pool3", True)
         weigh_on_vector(A3)

@@ -23,7 +23,7 @@ RUN = 8
 CH = 128
 HALF = H // 2
 WALK = 4
-EARLY_WORDS = 3 * T // 8
+EARLY_WORDS = T // 2
 POOL_SCALE = 0.0625
 
 B, A = 0, 1

@@ -22,7 +22,7 @@ SLOTS = 4
 RUN = 8
 CH = 128
 HALF = H // 2
-WALK = 4
+RUN_BYTES = 8
 EARLY_WORDS = T // 2
 POOL_SCALE = 0.0625
 
@@ -95,12 +95,12 @@ def tile_picked_bilpool_none_p_kernel(tc, x_words, x_scales, wa, wb, gt, gi, off
             nc.vector.transpose(turned[:], dealt[:])
             nc.vector.tensor_copy(gates[:], turned[:].rearrange("p (t i) -> p i t", i=QUAD)[:, 0:2, :])
 
-        def interleave(copy, words, slots):
-            copy(words.rearrange("p (c i) t -> p c t i", i=WALK), slots.rearrange("p t (c i) -> p c t i", i=WALK))
+        def interleave(copy, words, slots, walk):
+            copy(words.rearrange("p (c i) t -> p c t i", i=walk), slots.rearrange("p t (c i) -> p c t i", i=walk))
 
         def round_weights(chunk):
             w_bf[chunk] = keep.tile([P, CH, SLOTS], BF16, name=tag("w_bf", chunk), align_bytes=64)
-            interleave(nc.scalar.copy, w_bf[chunk][:], w_raw[chunk][:])
+            interleave(nc.scalar.copy, w_bf[chunk][:], w_raw[chunk][:], RUN_BYTES // 4)
 
         def project(chunk):
             codes = keep.tile([P, CH], U32, name=tag("w_codes", chunk), align_bytes=64)
@@ -124,7 +124,7 @@ def tile_picked_bilpool_none_p_kernel(tc, x_words, x_scales, wa, wb, gt, gi, off
 
         def interleave_weighed(chunk):
             side, i = chunk
-            interleave(nc.vector.tensor_copy, z_bf[side][:, columns(i, i + 1), :], weighed[chunk][:])
+            interleave(nc.vector.tensor_copy, z_bf[side][:, columns(i, i + 1), :], weighed[chunk][:], RUN_BYTES // 2)
 
         def quantise_z(first, last):
             side, cols = first[0], columns(first[1], last[1] + 1)

@@ -178,17 +178,18 @@ def tile_picked_bilpool_none_p_kernel(tc, x_words, x_scales, wa, wb, gt, gi, off
         round_weights(A2)
         quantise_z(B0, B1)
         interleave_weighed(A1)
+        project(A2)
         round_weights(A3)
         weigh_on_scalar(B3)
+        weigh_on_scalar(A2)
         weigh_on_vector(B2)
-        project(A2)
+        project(A3)
         quantise_z(A0, A1)
         pool_first_quarter("pool0")
-        project(A3)
-        weigh_on_vector(A2)
         interleave_weighed(B3)
-        quantise_z(A2, A2)
+        interleave_weighed(A2)
         quantise_z(B2, B3)
+        quantise_z(A2, A2)
         pool_piece(0, 1, "pool1", True)
         pool_piece(2, 0, "pool3", True)
         weigh_on_vector(A3)

@@ -60,8 +60,7 @@ def tile_picked_bilpool_none_p_kernel(tc, x_words, x_scales, wa, wb, gt, gi, off
             nc.sync.dma_start(raw[:], (wb, wa)[side].rearrange("(p t) n -> p t n", t=SLOTS)[:, :, columns(i, i + 1)])
             w_raw[chunk] = raw
 
-        nc.vector.memset(scale_table[:, 0 : T // 2].bitcast(I32), 0)
-        nc.gpsimd.memset(scale_table[:, T // 2 : T].bitcast(I32), 0)
+        nc.vector.memset(scale_table[:].bitcast(I32), 0)
         nc.vector.memset(gate_rows[:], 0.0)
         load_words(slice(0, EARLY_WORDS))
         nc.sync.dma_start(offsets[:], offs)

@@ -79,8 +79,9 @@ def tile_picked_bilpool_none_p_kernel(tc, x_words, x_scales, wa, wb, gt, gi, off
         nc.vector.tensor_copy(picked_bytes[:], scale_table[:].indirect(offsets[:]))
         nc.vector.tensor_copy(x_codes[:].rearrange("p t (j r) -> p j t r", r=RUN), word_table[:].bitcast(U32).indirect(offsets[:]))
 
-        gates = keep.tile([P, 2, SLOTS], F32, name="gates")
-        z_bf = [keep.tile([P, H, SLOTS], BF16, name="z_bf%d" % side, align_bytes=64) for side in (B, A)]
+        turned = keep.tile([P, P], F32, name="gate_turned", align_bytes=64)
+        gates = turned[:].rearrange("p (t i) -> p i t", i=QUAD)
+        z_bf = {}
         z_codes = [keep.tile([P, H], U32, name="z_codes%d" % side, align_bytes=64) for side in (B, A)]
         z_planes = [keep.tile([P, H], U8, name="z_planes%d" % side, align_bytes=64) for side in (B, A)]
         w_bf = {}
@@ -89,10 +90,18 @@ def tile_picked_bilpool_none_p_kernel(tc, x_words, x_scales, wa, wb, gt, gi, off
 
         def deal_gates():
             dealt = keep.tile([P, P], F32, name=tag("w_bf", B0), align_bytes=64)
-            turned = keep.tile([P, P], F32, name="gate_turned", align_bytes=64)
             nc.vector.tensor_copy(dealt[:].rearrange("p (t j r) -> p t j r", t=SLOTS, r=RUN), gate_rows[:].rearrange("p (j t r) -> p t j r", t=SLOTS, r=RUN))
             nc.vector.transpose(turned[:], dealt[:])
-            nc.vector.tensor_copy(gates[:], turned[:].rearrange("p (t i) -> p i t", i=QUAD)[:, 0:2, :])
+
+        def stage_z(chunks, after=None, kind="w_raw"):
+            name = tag("z_bf", chunks[0]) if after is None else tag(kind, after)
+            staged = keep.tile([P, len(chunks) * CH, SLOTS], BF16, name=name, align_bytes=64)
+            for n, chunk in enumerate(chunks):
+                z_bf[chunk] = (staged, n)
+
+        def z_words(chunk):
+            staged, n = z_bf[chunk]
+            return staged[:, columns(n, n + 1), :]
 
         def interleave(copy, words, slots, walk):
             copy(words.rearrange("p (c i) t -> p c t i", i=walk), slots.rearrange("p t (c i) -> p c t i", i=walk))
@@ -112,9 +121,8 @@ def tile_picked_bilpool_none_p_kernel(tc, x_words, x_scales, wa, wb, gt, gi, off
             projected[chunk] = acc
 
         def weigh_on_vector(chunk):
-            side, i = chunk
-            nc.vector.tensor_tensor(z_bf[side][:, columns(i, i + 1), :], projected[chunk][:].rearrange("p t n -> p n t"),
-                                    gates[:, side, :].unsqueeze(1).to_broadcast([P, CH, SLOTS]), MULT)
+            nc.vector.tensor_tensor(z_words(chunk), projected[chunk][:].rearrange("p t n -> p n t"),
+                                    gates[:, chunk[0], :].unsqueeze(1).to_broadcast([P, CH, SLOTS]), MULT)
 
         def weigh_on_scalar(chunk):
             weighed[chunk] = keep.tile([P, SLOTS, CH], BF16, name=tag("weighed", chunk), align_bytes=64)
@@ -122,13 +130,12 @@ def tile_picked_bilpool_none_p_kernel(tc, x_words, x_scales, wa, wb, gt, gi, off
                 nc.scalar.activation(weighed[chunk][:, t, :], projected[chunk][:, t, :], COPY, scale=gates[:, chunk[0], t : t + 1])
 
         def interleave_weighed(chunk):
-            side, i = chunk
-            interleave(nc.vector.tensor_copy, z_bf[side][:, columns(i, i + 1), :], weighed[chunk][:], RUN_BYTES // 2)
+            interleave(nc.vector.tensor_copy, z_words(chunk), weighed[chunk][:], RUN_BYTES // 2)
 
         def quantise_z(first, last):
             side, cols = first[0], columns(first[1], last[1] + 1)
             nc.vector.quantize_mx(out=z_codes[side][:, cols].bitcast(FP8X4), scales=z_planes[side][:, cols],
-                                  in_=z_bf[side][:, cols, :].rearrange("p n t -> p (n t)"))
+                                  in_=z_bf[first][0][:, columns(z_bf[first][1], z_bf[last][1] + 1), :].rearrange("p n t -> p (n t)"))
 
         def pool_pass(acc, i, half):
             rows, cols = columns(i, i + 1), slice(half * HALF, (half + 1) * HALF)
@@ -143,7 +150,7 @@ def tile_picked_bilpool_none_p_kernel(tc, x_words, x_scales, wa, wb, gt, gi, off
             nc.scalar.activation(res[:], acc[:], COPY, scale=POOL_SCALE)
             nc.sync.dma_start(out[0:HALF, 0:HALF].rearrange("(i p) n -> p i n", i=2), res[:])
 
-        def pool_piece(i, half, bank, on_scalar):
+        def pool_piece(i, half, bank, on_scalar, queue=nc.sync):
             acc = psum.tile([P, HALF], F32, name=bank)
             pool_pass(acc[:], i, half)
             res = keep.tile([P, HALF], F32, name="res%d_%d" % (i, half))
@@ -151,7 +158,7 @@ def tile_picked_bilpool_none_p_kernel(tc, x_words, x_scales, wa, wb, gt, gi, off
                 nc.scalar.activation(res[:], acc[:], COPY, scale=POOL_SCALE)
             else:
                 nc.vector.tensor_scalar(res[:], acc[:], POOL_SCALE, None, MULT)
-            nc.sync.dma_start(out[columns(i, i + 1), half * HALF : (half + 1) * HALF], res[:])
+            queue.dma_start(out[columns(i, i + 1), half * HALF : (half + 1) * HALF], res[:])
 
         round_weights(B0)
         x_planes = keep.tile([P, SLOTS, P], U8, name=tag("w_raw", B0), align_bytes=64)
@@ -165,6 +172,7 @@ def tile_picked_bilpool_none_p_kernel(tc, x_words, x_scales, wa, wb, gt, gi, off
             round_weights(chunk)
             project(chunk)
         round_weights(A1)
+        stage_z((B0, B1))
         weigh_on_vector(B0)
         project(A1)
         round_weights(B2)
@@ -172,6 +180,7 @@ def tile_picked_bilpool_none_p_kernel(tc, x_words, x_scales, wa, wb, gt, gi, off
         project(B2)
         round_weights(B3)
         weigh_on_scalar(A1)
+        stage_z((A0, A1))
         weigh_on_vector(A0)
         project(B3)
         round_weights(A2)
@@ -181,19 +190,22 @@ def tile_picked_bilpool_none_p_kernel(tc, x_words, x_scales, wa, wb, gt, gi, off
         round_weights(A3)
         weigh_on_scalar(B3)
         weigh_on_scalar(A2)
+        stage_z((B2, B3))
         weigh_on_vector(B2)
         project(A3)
         quantise_z(A0, A1)
         pool_first_quarter("pool0")
         interleave_weighed(B3)
+        stage_z((A2,))
         interleave_weighed(A2)
         quantise_z(B2, B3)
         quantise_z(A2, A2)
         pool_piece(0, 1, "pool1", True)
         pool_piece(2, 0, "pool3", True)
+        stage_z((A3,), A2, "weighed")
         weigh_on_vector(A3)
         pool_piece(1, 1, "pool2", False)
         quantise_z(A3, A3)
         pool_piece(2, 1, "proj0", False)
-        pool_piece(3, 0, "proj1", True)
+        pool_piece(3, 0, "proj1", True, nc.scalar)
         pool_piece(3, 1, "pool0", False)

@@ -48,7 +48,7 @@ def tile_picked_bilpool_none_p_kernel(tc, x_words, x_scales, wa, wb, gt, gi, off
         offsets = keep.tile([P, S // 16], U16, name="offsets")
         scale_table = keep.tile([P, T], U8, name="scale_table", align_bytes=64)
         word_table = keep.tile([P, T], I32, name="word_table", align_bytes=64)
-        gate_rows = keep.tile([P, P], F32, name="gate_rows", align_bytes=64)
+        gate_rows = keep.tile([P, QUAD], F32, name="gate_rows", align_bytes=64)
         w_raw = {}
 
         def load_words(cols):
@@ -70,17 +70,17 @@ def tile_picked_bilpool_none_p_kernel(tc, x_words, x_scales, wa, wb, gt, gi, off
         load_weights(B0)
         load_weights(B1)
         for side, gate in ((B, gi), (A, gt)):
-            nc.sync.dma_start(gate_rows[side:P:QUAD, :], gate.rearrange("(q e) o -> q (e o)", q=QUADS))
+            nc.sync.dma_start(gate_rows[side:P:RUN, :].rearrange("m (a r) -> m a r", r=RUN), gate.rearrange("(a m r) o -> m a (r o)", a=QUADS, r=RUN))
         for chunk in ORDER[2:]:
             load_weights(chunk)
 
         picked_bytes = keep.tile([P, S], U8, name="picked_bytes", align_bytes=64)
         x_codes = keep.tile([P, SLOTS, P], U32, name="x_codes", align_bytes=64)
         nc.vector.tensor_copy(picked_bytes[:], scale_table[:].indirect(offsets[:]))
-        nc.vector.tensor_copy(x_codes[:].rearrange("p t (j r) -> p j t r", r=RUN), word_table[:].bitcast(U32).indirect(offsets[:]))
+        nc.vector.tensor_copy(x_codes[:].rearrange("p t (q a r) -> p a q t r", q=QUADS, r=RUN), word_table[:].bitcast(U32).indirect(offsets[:]))
 
-        turned = keep.tile([P, P], F32, name="gate_turned", align_bytes=64)
-        gates = turned[:].rearrange("p (t i) -> p i t", i=QUAD)
+        turned = keep.tile([P, QUAD], F32, name="gate_turned", align_bytes=64)
+        gates = turned[:].rearrange("p (t i) -> p i t", i=RUN)
         z_bf = {}
         z_codes = [keep.tile([P, H], U32, name="z_codes%d" % side, align_bytes=64) for side in (B, A)]
         z_planes = [keep.tile([P, H], U8, name="z_planes%d" % side, align_bytes=64) for side in (B, A)]
@@ -89,9 +89,7 @@ def tile_picked_bilpool_none_p_kernel(tc, x_words, x_scales, wa, wb, gt, gi, off
         weighed = {}
 
         def deal_gates():
-            dealt = keep.tile([P, P], F32, name=tag("w_bf", B0), align_bytes=64)
-            nc.vector.tensor_copy(dealt[:].rearrange("p (t j r) -> p t j r", t=SLOTS, r=RUN), gate_rows[:].rearrange("p (j t r) -> p t j r", t=SLOTS, r=RUN))
-            nc.vector.transpose(turned[:], dealt[:])
+            nc.vector.transpose(turned[:], gate_rows[:])
 
         def stage_z(chunks, after=None, kind="w_raw"):
             name = tag("z_bf", chunks[0]) if after is None else tag(kind, after)
@@ -163,8 +161,8 @@ def tile_picked_bilpool_none_p_kernel(tc, x_words, x_scales, wa, wb, gt, gi, off
         round_weights(B0)
         x_planes = keep.tile([P, SLOTS, P], U8, name=tag("w_raw", B0), align_bytes=64)
         nc.vector.tensor_copy(
-            x_planes[:].bitcast(I32).rearrange("p t (j w) -> p t j w", w=RUN // 4),
-            picked_bytes[:].bitcast(I32).rearrange("p (j t w) -> p t j w", t=SLOTS, w=RUN // 4),
+            x_planes[:].bitcast(I32).rearrange("p t (q a w) -> p t q a w", q=QUADS, w=RUN // 4),
+            picked_bytes[:].bitcast(I32).rearrange("p (a q t w) -> p t q a w", q=QUADS, t=SLOTS, w=RUN // 4),
         )
         project(B0)
         deal_gates()
@@ -172,7 +170,7 @@ def tile_picked_bilpool_none_p_kernel(tc, x_words, x_scales, wa, wb, gt, gi, off
             round_weights(chunk)
             project(chunk)
         round_weights(A1)
-        stage_z((B0, B1))
+        stage_z((B0, B1), A0)
         weigh_on_vector(B0)
         project(A1)
         round_weights(B2)

@@ -79,8 +79,7 @@ def tile_picked_bilpool_none_p_kernel(tc, x_words, x_scales, wa, wb, gt, gi, off
         nc.vector.tensor_copy(picked_bytes[:], scale_table[:].indirect(offsets[:]))
         nc.vector.tensor_copy(x_codes[:].rearrange("p t (q a r) -> p a q t r", q=QUADS, r=RUN), word_table[:].bitcast(U32).indirect(offsets[:]))
 
-        turned = keep.tile([P, QUAD], F32, name="gate_turned", align_bytes=64)
-        gates = turned[:].rearrange("p (t i) -> p i t", i=RUN)
+        gates = keep.tile([P, 2, SLOTS], F32, name="gates")
         z_bf = {}
         z_codes = [keep.tile([P, H], U32, name="z_codes%d" % side, align_bytes=64) for side in (B, A)]
         z_planes = [keep.tile([P, H], U8, name="z_planes%d" % side, align_bytes=64) for side in (B, A)]
@@ -89,7 +88,9 @@ def tile_picked_bilpool_none_p_kernel(tc, x_words, x_scales, wa, wb, gt, gi, off
         weighed = {}
 
         def deal_gates():
+            turned = keep.tile([P, QUAD], F32, name=tag("w_bf", B0), align_bytes=64)
             nc.vector.transpose(turned[:], gate_rows[:])
+            nc.vector.tensor_copy(gates[:], turned[:].rearrange("p (t i) -> p i t", i=RUN)[:, 0:2, :])
 
         def stage_z(chunks, after=None, kind="w_raw"):
             name = tag("z_bf", chunks[0]) if after is None else tag(kind, after)

@@ -20,6 +20,7 @@ QUAD = 32
 QUADS = P // QUAD
 SLOTS = 4
 RUN = 8
+GROUPS = QUAD // RUN
 CH = 128
 HALF = H // 2
 RUN_BYTES = 8
@@ -70,14 +71,14 @@ def tile_picked_bilpool_none_p_kernel(tc, x_words, x_scales, wa, wb, gt, gi, off
         load_weights(B0)
         load_weights(B1)
         for side, gate in ((B, gi), (A, gt)):
-            nc.sync.dma_start(gate_rows[side:P:RUN, :].rearrange("m (a r) -> m a r", r=RUN), gate.rearrange("(a m r) o -> m a (r o)", a=QUADS, r=RUN))
+            nc.sync.dma_start(gate_rows[side:P:RUN, :].rearrange("m (g r) -> m g r", r=RUN), gate.rearrange("(g m r) o -> m g (r o)", g=GROUPS, r=RUN))
         for chunk in ORDER[2:]:
             load_weights(chunk)
 
         picked_bytes = keep.tile([P, S], U8, name="picked_bytes", align_bytes=64)
         x_codes = keep.tile([P, SLOTS, P], U32, name="x_codes", align_bytes=64)
         nc.vector.tensor_copy(picked_bytes[:], scale_table[:].indirect(offsets[:]))
-        nc.vector.tensor_copy(x_codes[:].rearrange("p t (q a r) -> p a q t r", q=QUADS, r=RUN), word_table[:].bitcast(U32).indirect(offsets[:]))
+        nc.vector.tensor_copy(x_codes[:].rearrange("p t (q g r) -> p g q t r", q=QUADS, r=RUN), word_table[:].bitcast(U32).indirect(offsets[:]))
 
         gates = keep.tile([P, 2, SLOTS], F32, name="gates")
         z_bf = {}
@@ -92,8 +93,7 @@ def tile_picked_bilpool_none_p_kernel(tc, x_words, x_scales, wa, wb, gt, gi, off
             nc.vector.transpose(turned[:], gate_rows[:])
             nc.vector.tensor_copy(gates[:], turned[:].rearrange("p (t i) -> p i t", i=RUN)[:, 0:2, :])
 
-        def stage_z(chunks, after=None, kind="w_raw"):
-            name = tag("z_bf", chunks[0]) if after is None else tag(kind, after)
+        def stage_z(chunks, name):
             staged = keep.tile([P, len(chunks) * CH, SLOTS], BF16, name=name, align_bytes=64)
             for n, chunk in enumerate(chunks):
                 z_bf[chunk] = (staged, n)
@@ -134,7 +134,7 @@ def tile_picked_bilpool_none_p_kernel(tc, x_words, x_scales, wa, wb, gt, gi, off
         def quantise_z(first, last):
             side, cols = first[0], columns(first[1], last[1] + 1)
             nc.vector.quantize_mx(out=z_codes[side][:, cols].bitcast(FP8X4), scales=z_planes[side][:, cols],
-                                  in_=z_bf[first][0][:, columns(z_bf[first][1], z_bf[last][1] + 1), :].rearrange("p n t -> p (n t)"))
+                                  in_=z_bf[first][0][:].rearrange("p n t -> p (n t)"))
 
         def pool_pass(acc, i, half):
             rows, cols = columns(i, i + 1), slice(half * HALF, (half + 1) * HALF)
@@ -149,7 +149,7 @@ def tile_picked_bilpool_none_p_kernel(tc, x_words, x_scales, wa, wb, gt, gi, off
             nc.scalar.activation(res[:], acc[:], COPY, scale=POOL_SCALE)
             nc.sync.dma_start(out[0:HALF, 0:HALF].rearrange("(i p) n -> p i n", i=2), res[:])
 
-        def pool_piece(i, half, bank, on_scalar, queue=nc.sync):
+        def pool_piece(i, half, bank, on_scalar):
             acc = psum.tile([P, HALF], F32, name=bank)
             pool_pass(acc[:], i, half)
             res = keep.tile([P, HALF], F32, name="res%d_%d" % (i, half))
@@ -157,13 +157,13 @@ def tile_picked_bilpool_none_p_kernel(tc, x_words, x_scales, wa, wb, gt, gi, off
                 nc.scalar.activation(res[:], acc[:], COPY, scale=POOL_SCALE)
             else:
                 nc.vector.tensor_scalar(res[:], acc[:], POOL_SCALE, None, MULT)
-            queue.dma_start(out[columns(i, i + 1), half * HALF : (half + 1) * HALF], res[:])
+            nc.sync.dma_start(out[columns(i, i + 1), half * HALF : (half + 1) * HALF], res[:])
 
         round_weights(B0)
         x_planes = keep.tile([P, SLOTS, P], U8, name=tag("w_raw", B0), align_bytes=64)
         nc.vector.tensor_copy(
-            x_planes[:].bitcast(I32).rearrange("p t (q a w) -> p t q a w", q=QUADS, w=RUN // 4),
-            picked_bytes[:].bitcast(I32).rearrange("p (a q t w) -> p t q a w", q=QUADS, t=SLOTS, w=RUN // 4),
+            x_planes[:].bitcast(I32).rearrange("p t (q g w) -> p t q g w", q=QUADS, w=RUN // 4),
+            picked_bytes[:].bitcast(I32).rearrange("p (g q t w) -> p t q g w", q=QUADS, t=SLOTS, w=RUN // 4),
         )
         project(B0)
         deal_gates()
@@ -171,7 +171,7 @@ def tile_picked_bilpool_none_p_kernel(tc, x_words, x_scales, wa, wb, gt, gi, off
             round_weights(chunk)
             project(chunk)
         round_weights(A1)
-        stage_z((B0, B1), A0)
+        stage_z((B0, B1), tag("w_raw", A0))
         weigh_on_vector(B0)
         project(A1)
         round_weights(B2)
@@ -179,7 +179,7 @@ def tile_picked_bilpool_none_p_kernel(tc, x_words, x_scales, wa, wb, gt, gi, off
         project(B2)
         round_weights(B3)
         weigh_on_scalar(A1)
-        stage_z((A0, A1))
+        stage_z((A0, A1), tag("z_bf", A0))
         weigh_on_vector(A0)
         project(B3)
         round_weights(A2)
@@ -188,23 +188,23 @@ def tile_picked_bilpool_none_p_kernel(tc, x_words, x_scales, wa, wb, gt, gi, off
         project(A2)
         round_weights(A3)
         weigh_on_scalar(B3)
-        weigh_on_scalar(A2)
-        stage_z((B2, B3))
+        stage_z((B2, B3), tag("z_bf", B2))
         weigh_on_vector(B2)
-        project(A3)
         quantise_z(A0, A1)
         pool_first_quarter("pool0")
+        weigh_on_scalar(A2)
+        project(A3)
         interleave_weighed(B3)
-        stage_z((A2,))
+        stage_z((A2,), tag("z_bf", A2))
         interleave_weighed(A2)
         quantise_z(B2, B3)
         quantise_z(A2, A2)
         pool_piece(0, 1, "pool1", True)
         pool_piece(2, 0, "pool3", True)
-        stage_z((A3,), A2, "weighed")
+        stage_z((A3,), tag("weighed", A2))
         weigh_on_vector(A3)
         pool_piece(1, 1, "pool2", False)
         quantise_z(A3, A3)
         pool_piece(2, 1, "proj0", False)
-        pool_piece(3, 0, "proj1", True, nc.scalar)
+        pool_piece(3, 0, "proj1", True)
         pool_piece(3, 1, "pool0", False)

@@ -136,75 +136,63 @@ def tile_picked_bilpool_none_p_kernel(tc, x_words, x_scales, wa, wb, gt, gi, off
             nc.vector.quantize_mx(out=z_codes[side][:, cols].bitcast(FP8X4), scales=z_planes[side][:, cols],
                                   in_=z_bf[first][0][:].rearrange("p n t -> p (n t)"))
 
-        def pool_pass(acc, i, half):
-            rows, cols = columns(i, i + 1), slice(half * HALF, (half + 1) * HALF)
-            nc.tensor.matmul_mx(out=acc, lhsT=z_codes[A][:, rows].bitcast(FP8X4), lhsT_scale=z_planes[A][:, rows],
-                                rhs=z_codes[B][:, cols].bitcast(FP8X4), rhs_scale=z_planes[B][:, cols], start=True, stop=True)
-
-        def pool_first_quarter(bank):
-            acc = psum.tile([P, 2, HALF], F32, name=bank)
-            for i in range(2):
-                pool_pass(acc[:, i, :], i, 0)
-            res = keep.tile([P, 2, HALF], F32, name="res_quarter")
-            nc.scalar.activation(res[:], acc[:], COPY, scale=POOL_SCALE)
-            nc.sync.dma_start(out[0:HALF, 0:HALF].rearrange("(i p) n -> p i n", i=2), res[:])
-
-        def pool_piece(i, half, bank, on_scalar):
-            acc = psum.tile([P, HALF], F32, name=bank)
-            pool_pass(acc[:], i, half)
-            res = keep.tile([P, HALF], F32, name="res%d_%d" % (i, half))
+        def pool(rows, cols, bank, on_scalar):
+            n, width = rows[1] - rows[0], (cols[1] - cols[0]) * CH
+            acc = psum.tile([P, n, width], F32, name=bank)
+            cs = columns(cols[0], cols[1])
+            for i in range(n):
+                rs = columns(rows[0] + i, rows[0] + i + 1)
+                nc.tensor.matmul_mx(out=acc[:, i, :], lhsT=z_codes[A][:, rs].bitcast(FP8X4), lhsT_scale=z_planes[A][:, rs],
+                                    rhs=z_codes[B][:, cs].bitcast(FP8X4), rhs_scale=z_planes[B][:, cs], start=True, stop=True)
+            res = keep.tile([P, n, width], F32, name="res%d_%d" % (rows[0], cols[0]))
             if on_scalar:
                 nc.scalar.activation(res[:], acc[:], COPY, scale=POOL_SCALE)
             else:
                 nc.vector.tensor_scalar(res[:], acc[:], POOL_SCALE, None, MULT)
-            nc.sync.dma_start(out[columns(i, i + 1), half * HALF : (half + 1) * HALF], res[:])
+            nc.sync.dma_start(out[columns(rows[0], rows[1]), cs].rearrange("(i p) n -> p i n", i=n), res[:])
+
+        def deal_bytes():
+            nc.vector.tensor_copy(
+                x_planes[:].bitcast(I32).rearrange("p t (q g w) -> p t q g w", q=QUADS, w=RUN // 4),
+                picked_bytes[:].bitcast(I32).rearrange("p (g q t w) -> p t q g w", q=QUADS, t=SLOTS, w=RUN // 4),
+            )
 
         round_weights(B0)
         x_planes = keep.tile([P, SLOTS, P], U8, name=tag("w_raw", B0), align_bytes=64)
-        nc.vector.tensor_copy(
-            x_planes[:].bitcast(I32).rearrange("p t (q g w) -> p t q g w", q=QUADS, w=RUN // 4),
-            picked_bytes[:].bitcast(I32).rearrange("p (g q t w) -> p t q g w", q=QUADS, t=SLOTS, w=RUN // 4),
-        )
+        deal_bytes()
+        for chunk in ORDER[1:]: round_weights(chunk)
         project(B0)
         deal_gates()
-        for chunk in (B1, A0):
-            round_weights(chunk)
-            project(chunk)
-        round_weights(A1)
+        project(B1)
+        project(A0)
         stage_z((B0, B1), tag("w_raw", A0))
         weigh_on_vector(B0)
         project(A1)
-        round_weights(B2)
         weigh_on_vector(B1)
         project(B2)
-        round_weights(B3)
-        weigh_on_scalar(A1)
-        stage_z((A0, A1), tag("z_bf", A0))
+        stage_z((A0, A1), "z_a01")
         weigh_on_vector(A0)
         project(B3)
-        round_weights(A2)
-        quantise_z(B0, B1)
-        interleave_weighed(A1)
         project(A2)
-        round_weights(A3)
         weigh_on_scalar(B3)
-        stage_z((B2, B3), tag("z_bf", B2))
-        weigh_on_vector(B2)
-        quantise_z(A0, A1)
-        pool_first_quarter("pool0")
         weigh_on_scalar(A2)
+        weigh_on_vector(A1)
         project(A3)
+        quantise_z(B0, B1)
+        quantise_z(A0, A1)
+        pool((0, 2), (0, 2), "pool0", True)
+        for chunk in (B2, B3, A2, A3): stage_z((chunk,), tag("z_bf", chunk))
+        weigh_on_vector(B2)
         interleave_weighed(B3)
-        stage_z((A2,), tag("z_bf", A2))
+        quantise_z(B2, B2)
+        pool((0, 2), (2, 3), "pool1", True)
         interleave_weighed(A2)
-        quantise_z(B2, B3)
+        quantise_z(B3, B3)
+        pool((0, 2), (3, 4), "pool2", True)
         quantise_z(A2, A2)
-        pool_piece(0, 1, "pool1", True)
-        pool_piece(2, 0, "pool3", True)
-        stage_z((A3,), tag("weighed", A2))
+        pool((2, 3), (0, 2), "pool3", True)
         weigh_on_vector(A3)
-        pool_piece(1, 1, "pool2", False)
+        pool((2, 3), (2, 4), "proj0", False)
         quantise_z(A3, A3)
-        pool_piece(2, 1, "proj0", False)
-        pool_piece(3, 0, "proj1", True)
-        pool_piece(3, 1, "pool0", False)
+        pool((3, 4), (0, 2), "proj1", True)
+        pool((3, 4), (2, 4), "pool0", False)

@@ -173,16 +173,16 @@ def tile_picked_bilpool_none_p_kernel(tc, x_words, x_scales, wa, wb, gt, gi, off
         stage_z((A0, A1), "z_a01")
         weigh_on_vector(A0)
         project(B3)
-        project(A2)
         weigh_on_scalar(B3)
-        weigh_on_scalar(A2)
         weigh_on_vector(A1)
-        project(A3)
+        project(A2)
+        weigh_on_scalar(A2)
         quantise_z(B0, B1)
         quantise_z(A0, A1)
         pool((0, 2), (0, 2), "pool0", True)
         for chunk in (B2, B3, A2, A3): stage_z((chunk,), tag("z_bf", chunk))
         weigh_on_vector(B2)
+        project(A3)
         interleave_weighed(B3)
         quantise_z(B2, B2)
         pool((0, 2), (2, 3), "pool1", True)

@@ -70,17 +70,18 @@ def tile_picked_bilpool_none_p_kernel(tc, x_words, x_scales, wa, wb, gt, gi, off
         load_words(slice(EARLY_WORDS, T))
         load_weights(B0)
         load_weights(B1)
+        load_weights(A0)
         for side, gate in ((B, gi), (A, gt)):
             nc.sync.dma_start(gate_rows[side:P:RUN, :].rearrange("m (g r) -> m g r", r=RUN), gate.rearrange("(g m r) o -> m g (r o)", g=GROUPS, r=RUN))
-        for chunk in ORDER[2:]:
+        for chunk in ORDER[3:]:
             load_weights(chunk)
 
-        picked_bytes = keep.tile([P, S], U8, name="picked_bytes", align_bytes=64)
+        x_planes = keep.tile([P, SLOTS, P], U8, name="x_planes", align_bytes=64)
         x_codes = keep.tile([P, SLOTS, P], U32, name="x_codes", align_bytes=64)
-        nc.vector.tensor_copy(picked_bytes[:], scale_table[:].indirect(offsets[:]))
+        nc.vector.tensor_copy(x_planes[:].rearrange("p t (q g r) -> p g q t r", q=QUADS, r=RUN), scale_table[:].indirect(offsets[:]))
         nc.vector.tensor_copy(x_codes[:].rearrange("p t (q g r) -> p g q t r", q=QUADS, r=RUN), word_table[:].bitcast(U32).indirect(offsets[:]))
 
-        gates = keep.tile([P, 2, SLOTS], F32, name="gates")
+        gates = {}
         z_bf = {}
         z_codes = [keep.tile([P, H], U32, name="z_codes%d" % side, align_bytes=64) for side in (B, A)]
         z_planes = [keep.tile([P, H], U8, name="z_planes%d" % side, align_bytes=64) for side in (B, A)]
@@ -91,7 +92,8 @@ def tile_picked_bilpool_none_p_kernel(tc, x_words, x_scales, wa, wb, gt, gi, off
         def deal_gates():
             turned = keep.tile([P, QUAD], F32, name=tag("w_bf", B0), align_bytes=64)
             nc.vector.transpose(turned[:], gate_rows[:])
-            nc.vector.tensor_copy(gates[:], turned[:].rearrange("p (t i) -> p i t", i=RUN)[:, 0:2, :])
+            for side in (B, A):
+                gates[side] = turned[:, side:QUAD:RUN]
 
         def stage_z(chunks, name):
             staged = keep.tile([P, len(chunks) * CH, SLOTS], BF16, name=name, align_bytes=64)
@@ -121,12 +123,12 @@ def tile_picked_bilpool_none_p_kernel(tc, x_words, x_scales, wa, wb, gt, gi, off
 
         def weigh_on_vector(chunk):
             nc.vector.tensor_tensor(z_words(chunk), projected[chunk][:].rearrange("p t n -> p n t"),
-                                    gates[:, chunk[0], :].unsqueeze(1).to_broadcast([P, CH, SLOTS]), MULT)
+                                    gates[chunk[0]].unsqueeze(1).to_broadcast([P, CH, SLOTS]), MULT)
 
         def weigh_on_scalar(chunk):
             weighed[chunk] = keep.tile([P, SLOTS, CH], BF16, name=tag("weighed", chunk), align_bytes=64)
             for t in range(SLOTS):
-                nc.scalar.activation(weighed[chunk][:, t, :], projected[chunk][:, t, :], COPY, scale=gates[:, chunk[0], t : t + 1])
+                nc.scalar.activation(weighed[chunk][:, t, :], projected[chunk][:, t, :], COPY, scale=gates[chunk[0]][:, t : t + 1])
 
         def interleave_weighed(chunk):
             interleave(nc.vector.tensor_copy, z_words(chunk), weighed[chunk][:], RUN_BYTES // 2)
@@ -151,20 +153,12 @@ def tile_picked_bilpool_none_p_kernel(tc, x_words, x_scales, wa, wb, gt, gi, off
                 nc.vector.tensor_scalar(res[:], acc[:], POOL_SCALE, None, MULT)
             nc.sync.dma_start(out[columns(rows[0], rows[1]), cs].rearrange("(i p) n -> p i n", i=n), res[:])
 
-        def deal_bytes():
-            nc.vector.tensor_copy(
-                x_planes[:].bitcast(I32).rearrange("p t (q g w) -> p t q g w", q=QUADS, w=RUN // 4),
-                picked_bytes[:].bitcast(I32).rearrange("p (g q t w) -> p t q g w", q=QUADS, t=SLOTS, w=RUN // 4),
-            )
-
         round_weights(B0)
-        x_planes = keep.tile([P, SLOTS, P], U8, name=tag("w_raw", B0), align_bytes=64)
-        deal_bytes()
         for chunk in ORDER[1:]: round_weights(chunk)
         project(B0)
-        deal_gates()
         project(B1)
         project(A0)
+        deal_gates()
         stage_z((B0, B1), tag("w_raw", A0))
         weigh_on_vector(B0)
         project(A1)

@@ -83,8 +83,12 @@ def tile_picked_bilpool_none_p_kernel(tc, x_words, x_scales, wa, wb, gt, gi, off
 
         gates = {}
         z_bf = {}
-        z_codes = [keep.tile([P, H], U32, name="z_codes%d" % side, align_bytes=64) for side in (B, A)]
-        z_planes = [keep.tile([P, H], U8, name="z_planes%d" % side, align_bytes=64) for side in (B, A)]
+        z_codes = keep.tile([P, len(ORDER) * CH], U32, name="z_codes", align_bytes=64)
+        z_planes = keep.tile([P, len(ORDER) * CH], U8, name="z_planes", align_bytes=64)
+
+        def z_columns(first, last):
+            return columns(ORDER.index(first), ORDER.index(last) + 1)
+
         w_bf = {}
         projected = {}
         weighed = {}
@@ -95,7 +99,7 @@ def tile_picked_bilpool_none_p_kernel(tc, x_words, x_scales, wa, wb, gt, gi, off
             for side in (B, A):
                 gates[side] = turned[:, side:QUAD:RUN]
 
-        def stage_z(chunks, name):
+        def stage_z(chunks, name, pool=keep):
             staged = keep.tile([P, len(chunks) * CH, SLOTS], BF16, name=name, align_bytes=64)
             for n, chunk in enumerate(chunks):
                 z_bf[chunk] = (staged, n)
@@ -107,19 +111,23 @@ def tile_picked_bilpool_none_p_kernel(tc, x_words, x_scales, wa, wb, gt, gi, off
         def interleave(copy, words, slots, walk):
             copy(words.rearrange("p (c i) t -> p c t i", i=walk), slots.rearrange("p t (c i) -> p c t i", i=walk))
 
-        def round_weights(chunk):
-            w_bf[chunk] = keep.tile([P, CH, SLOTS], BF16, name=tag("w_bf", chunk), align_bytes=64)
-            interleave(nc.scalar.copy, w_bf[chunk][:], w_raw[chunk][:], RUN_BYTES // 4)
+        def round_weights(*chunks):
+            w_bf[chunks[0]] = keep.tile([P, len(chunks) * CH, SLOTS], BF16, name=tag("w_bf", chunks[0]), align_bytes=64)
+            for n, chunk in enumerate(chunks):
+                nc.scalar.copy(w_bf[chunks[0]][:, columns(n, n + 1), :].rearrange("p (c i) (u e) -> p c u i e", i=4, e=2),
+                               w_raw[chunk][:].rearrange("p (u e) (c i) -> p c u i e", i=4, e=2))
 
-        def project(chunk):
-            codes = keep.tile([P, CH], U32, name=tag("w_codes", chunk), align_bytes=64)
-            planes = keep.tile([P, CH], U8, name=tag("w_planes", chunk), align_bytes=64)
-            nc.vector.quantize_mx(out=codes[:].bitcast(FP8X4), scales=planes[:], in_=w_bf[chunk][:].rearrange("p n t -> p (n t)"))
-            acc = psum.tile([P, SLOTS, CH], F32, name="proj%d" % (ORDER.index(chunk) % PROJ_BANKS))
-            for t in range(SLOTS):
-                nc.tensor.matmul_mx(out=acc[:, t, :], lhsT=x_codes[:, t, :].bitcast(FP8X4), lhsT_scale=x_planes[:, t, :],
-                                    rhs=codes[:].bitcast(FP8X4), rhs_scale=planes[:], start=True, stop=True)
-            projected[chunk] = acc
+        def project(*chunks, bank=None):
+            codes = keep.tile([P, len(chunks) * CH], U32, name=tag("w_codes", chunks[0]), align_bytes=64)
+            planes = keep.tile([P, len(chunks) * CH], U8, name=tag("w_planes", chunks[0]), align_bytes=64)
+            nc.vector.quantize_mx(out=codes[:].bitcast(FP8X4), scales=planes[:], in_=w_bf[chunks[0]][:].rearrange("p n t -> p (n t)"))
+            for n, chunk in enumerate(chunks):
+                cols = columns(n, n + 1)
+                acc = psum.tile([P, SLOTS, CH], F32, name=bank or "proj%d" % (ORDER.index(chunk) % PROJ_BANKS))
+                for t in range(SLOTS):
+                    nc.tensor.matmul_mx(out=acc[:, t, :], lhsT=x_codes[:, t, :].bitcast(FP8X4), lhsT_scale=x_planes[:, t, :],
+                                        rhs=codes[:, cols].bitcast(FP8X4), rhs_scale=planes[:, cols], start=True, stop=True)
+                projected[chunk] = acc
 
         def weigh_on_vector(chunk):
             nc.vector.tensor_tensor(z_words(chunk), projected[chunk][:].rearrange("p t n -> p n t"),
@@ -134,19 +142,22 @@ def tile_picked_bilpool_none_p_kernel(tc, x_words, x_scales, wa, wb, gt, gi, off
             interleave(nc.vector.tensor_copy, z_words(chunk), weighed[chunk][:], RUN_BYTES // 2)
 
         def quantise_z(first, last):
-            side, cols = first[0], columns(first[1], last[1] + 1)
-            nc.vector.quantize_mx(out=z_codes[side][:, cols].bitcast(FP8X4), scales=z_planes[side][:, cols],
+            cols = z_columns(first, last)
+            nc.vector.quantize_mx(out=z_codes[:, cols].bitcast(FP8X4), scales=z_planes[:, cols],
                                   in_=z_bf[first][0][:].rearrange("p n t -> p (n t)"))
 
-        def pool(rows, cols, bank, on_scalar):
+        def pool(rows, cols, bank, on_scalar, over=None):
             n, width = rows[1] - rows[0], (cols[1] - cols[0]) * CH
             acc = psum.tile([P, n, width], F32, name=bank)
             cs = columns(cols[0], cols[1])
             for i in range(n):
-                rs = columns(rows[0] + i, rows[0] + i + 1)
-                nc.tensor.matmul_mx(out=acc[:, i, :], lhsT=z_codes[A][:, rs].bitcast(FP8X4), lhsT_scale=z_planes[A][:, rs],
-                                    rhs=z_codes[B][:, cs].bitcast(FP8X4), rhs_scale=z_planes[B][:, cs], start=True, stop=True)
-            res = keep.tile([P, n, width], F32, name="res%d_%d" % (rows[0], cols[0]))
+                rs = z_columns((A, rows[0] + i), (A, rows[0] + i))
+                for c in range(cols[0], cols[1], 2):
+                    last = min(c + 2, cols[1])
+                    ms = z_columns((B, c), (B, last - 1))
+                    nc.tensor.matmul_mx(out=acc[:, i, columns(c - cols[0], last - cols[0])], lhsT=z_codes[:, rs].bitcast(FP8X4), lhsT_scale=z_planes[:, rs],
+                                        rhs=z_codes[:, ms].bitcast(FP8X4), rhs_scale=z_planes[:, ms], start=True, stop=True)
+            res = keep.tile([P, n, width], F32, name=over or "res%d_%d" % (rows[0], cols[0]), align_bytes=64)
             if on_scalar:
                 nc.scalar.activation(res[:], acc[:], COPY, scale=POOL_SCALE)
             else:
@@ -154,7 +165,9 @@ def tile_picked_bilpool_none_p_kernel(tc, x_words, x_scales, wa, wb, gt, gi, off
             nc.sync.dma_start(out[columns(rows[0], rows[1]), cs].rearrange("(i p) n -> p i n", i=n), res[:])
 
         round_weights(B0)
-        for chunk in ORDER[1:]: round_weights(chunk)
+        for chunk in (B1, A0, A1): round_weights(chunk)
+        round_weights(B3, B2)
+        for chunk in (A2, A3): round_weights(chunk)
         project(B0)
         project(B1)
         project(A0)
@@ -163,10 +176,9 @@ def tile_picked_bilpool_none_p_kernel(tc, x_words, x_scales, wa, wb, gt, gi, off
         weigh_on_vector(B0)
         project(A1)
         weigh_on_vector(B1)
-        project(B2)
         stage_z((A0, A1), "z_a01")
         weigh_on_vector(A0)
-        project(B3)
+        project(B3, B2)
         weigh_on_scalar(B3)
         weigh_on_vector(A1)
         project(A2)
@@ -180,13 +192,13 @@ def tile_picked_bilpool_none_p_kernel(tc, x_words, x_scales, wa, wb, gt, gi, off
         interleave_weighed(B3)
         quantise_z(B2, B2)
         pool((0, 2), (2, 3), "pool1", True)
-        interleave_weighed(A2)
         quantise_z(B3, B3)
         pool((0, 2), (3, 4), "pool2", True)
-        quantise_z(A2, A2)
-        pool((2, 3), (0, 2), "pool3", True)
         weigh_on_vector(A3)
-        pool((2, 3), (2, 4), "proj0", False)
+        interleave_weighed(A2)
         quantise_z(A3, A3)
-        pool((3, 4), (0, 2), "proj1", True)
-        pool((3, 4), (2, 4), "pool0", False)
+        quantise_z(A2, A2)
+        pool((3, 4), (0, 2), "pool3", True)
+        pool((3, 4), (2, 4), "proj0", False)
+        pool((2, 3), (0, 2), "proj1", True)
+        pool((2, 3), (2, 4), "pool0", False)

from contextlib import ExitStack

import concourse.mybir as mybir

K, T, S, H = 512, 2048, 512, 512
FLOPS = 2 * K * S * H * 2 + 2 * S * H * H

F32 = mybir.dt.float32
BF16 = mybir.dt.bfloat16
I32 = mybir.dt.int32
U32 = mybir.dt.uint32
U16 = mybir.dt.uint16
U8 = mybir.dt.uint8
FP8X4 = mybir.dt.float8_e4m3fn_x4
MULT = mybir.AluOpType.mult
COPY = mybir.ActivationFunctionType.Copy

P = 128
QUAD = 32
QUADS = P // QUAD
SLOTS = 4
RUN = 8
GROUPS = QUAD // RUN
CH = 128
HALF = H // 2
RUN_BYTES = 8
EARLY_WORDS = T // 2
POOL_SCALE = 0.0625

B, A = 0, 1
B0, B1, B2, B3 = [(B, i) for i in range(4)]
A0, A1, A2, A3 = [(A, i) for i in range(4)]
ORDER = (B0, B1, A0, A1, B2, B3, A2, A3)
PROJ_BANKS = 4


def tile_picked_bilpool_none_p_kernel(tc, x_words, x_scales, wa, wb, gt, gi, offs, out):
    nc = tc.nc
    with ExitStack() as ctx:
        keep = ctx.enter_context(tc.tile_pool(name="keep", bufs=1))
        psum = ctx.enter_context(tc.psum_pool(name="psum", bufs=1))

        def columns(first, last):
            return slice(first * CH, last * CH)

        def tag(name, chunk):
            return "%s_%d_%d" % (name, chunk[0], chunk[1])

        offsets = keep.tile([P, S // 16], U16, name="offsets")
        scale_table = keep.tile([P, T], U8, name="scale_table", align_bytes=64)
        word_table = keep.tile([P, T], I32, name="word_table", align_bytes=64)
        gate_rows = keep.tile([P, QUAD], F32, name="gate_rows", align_bytes=64)
        w_raw = {}

        def load_words(cols):
            nc.sync.dma_start(word_table[:, cols], x_words[0].rearrange("p n t -> p (n t)").bitcast(I32)[:, cols])

        def load_weights(chunk):
            side, i = chunk
            raw = keep.tile([P, SLOTS, CH], F32, name=tag("w_raw", chunk), align_bytes=64)
            nc.sync.dma_start(raw[:], (wb, wa)[side].rearrange("(p t) n -> p t n", t=SLOTS)[:, :, columns(i, i + 1)])
            w_raw[chunk] = raw

        nc.vector.memset(scale_table[:].bitcast(I32), 0)
        nc.vector.memset(gate_rows[:], 0.0)
        load_words(slice(0, EARLY_WORDS))
        nc.sync.dma_start(offsets[:], offs)
        for q in range(QUADS):
            nc.sync.dma_start(scale_table[QUAD * q : QUAD * q + 4, :].bitcast(I32), x_scales[0, 4 * q : 4 * q + 4, :].bitcast(I32))
        load_words(slice(EARLY_WORDS, T))
        load_weights(B0)
        load_weights(B1)
        load_weights(A0)
        for side, gate in ((B, gi), (A, gt)):
            nc.sync.dma_start(gate_rows[side:P:RUN, :].rearrange("m (g r) -> m g r", r=RUN), gate.rearrange("(g m r) o -> m g (r o)", g=GROUPS, r=RUN))
        for chunk in ORDER[3:]:
            load_weights(chunk)

        x_planes = keep.tile([P, SLOTS, P], U8, name="x_planes", align_bytes=64)
        x_codes = keep.tile([P, SLOTS, P], U32, name="x_codes", align_bytes=64)
        nc.vector.tensor_copy(x_planes[:].rearrange("p t (q g r) -> p g q t r", q=QUADS, r=RUN), scale_table[:].indirect(offsets[:]))
        nc.vector.tensor_copy(x_codes[:].rearrange("p t (q g r) -> p g q t r", q=QUADS, r=RUN), word_table[:].bitcast(U32).indirect(offsets[:]))

        gates = {}
        z_bf = {}
        z_codes = keep.tile([P, len(ORDER) * CH], U32, name="z_codes", align_bytes=64)
        z_planes = keep.tile([P, len(ORDER) * CH], U8, name="z_planes", align_bytes=64)

        def z_columns(first, last):
            return columns(ORDER.index(first), ORDER.index(last) + 1)

        w_bf = {}
        projected = {}
        weighed = {}

        def deal_gates():
            turned = keep.tile([P, QUAD], F32, name=tag("w_bf", B0), align_bytes=64)
            nc.vector.transpose(turned[:], gate_rows[:])
            for side in (B, A):
                gates[side] = turned[:, side:QUAD:RUN]

        def stage_z(chunks, name, pool=keep):
            staged = keep.tile([P, len(chunks) * CH, SLOTS], BF16, name=name, align_bytes=64)
            for n, chunk in enumerate(chunks):
                z_bf[chunk] = (staged, n)

        def z_words(chunk):
            staged, n = z_bf[chunk]
            return staged[:, columns(n, n + 1), :]

        def interleave(copy, words, slots, walk):
            copy(words.rearrange("p (c i) t -> p c t i", i=walk), slots.rearrange("p t (c i) -> p c t i", i=walk))

        def round_weights(*chunks):
            w_bf[chunks[0]] = keep.tile([P, len(chunks) * CH, SLOTS], BF16, name=tag("w_bf", chunks[0]), align_bytes=64)
            for n, chunk in enumerate(chunks):
                nc.scalar.copy(w_bf[chunks[0]][:, columns(n, n + 1), :].rearrange("p (c i) (u e) -> p c u i e", i=4, e=2),
                               w_raw[chunk][:].rearrange("p (u e) (c i) -> p c u i e", i=4, e=2))

        def project(*chunks, bank=None):
            codes = keep.tile([P, len(chunks) * CH], U32, name=tag("w_codes", chunks[0]), align_bytes=64)
            planes = keep.tile([P, len(chunks) * CH], U8, name=tag("w_planes", chunks[0]), align_bytes=64)
            nc.vector.quantize_mx(out=codes[:].bitcast(FP8X4), scales=planes[:], in_=w_bf[chunks[0]][:].rearrange("p n t -> p (n t)"))
            for n, chunk in enumerate(chunks):
                cols = columns(n, n + 1)
                acc = psum.tile([P, SLOTS, CH], F32, name=bank or "proj%d" % (ORDER.index(chunk) % PROJ_BANKS))
                for t in range(SLOTS):
                    nc.tensor.matmul_mx(out=acc[:, t, :], lhsT=x_codes[:, t, :].bitcast(FP8X4), lhsT_scale=x_planes[:, t, :],
                                        rhs=codes[:, cols].bitcast(FP8X4), rhs_scale=planes[:, cols], start=True, stop=True)
                projected[chunk] = acc

        def weigh_on_vector(chunk):
            nc.vector.tensor_tensor(z_words(chunk), projected[chunk][:].rearrange("p t n -> p n t"),
                                    gates[chunk[0]].unsqueeze(1).to_broadcast([P, CH, SLOTS]), MULT)

        def weigh_on_scalar(chunk):
            weighed[chunk] = keep.tile([P, SLOTS, CH], BF16, name=tag("weighed", chunk), align_bytes=64)
            for t in range(SLOTS):
                nc.scalar.activation(weighed[chunk][:, t, :], projected[chunk][:, t, :], COPY, scale=gates[chunk[0]][:, t : t + 1])

        def interleave_weighed(chunk):
            interleave(nc.vector.tensor_copy, z_words(chunk), weighed[chunk][:], RUN_BYTES // 2)

        def quantise_z(first, last):
            cols = z_columns(first, last)
            nc.vector.quantize_mx(out=z_codes[:, cols].bitcast(FP8X4), scales=z_planes[:, cols],
                                  in_=z_bf[first][0][:].rearrange("p n t -> p (n t)"))

        def pool(rows, cols, bank, on_scalar, over=None):
            n, width = rows[1] - rows[0], (cols[1] - cols[0]) * CH
            acc = psum.tile([P, n, width], F32, name=bank)
            cs = columns(cols[0], cols[1])
            for i in range(n):
                rs = z_columns((A, rows[0] + i), (A, rows[0] + i))
                for c in range(cols[0], cols[1], 2):
                    last = min(c + 2, cols[1])
                    ms = z_columns((B, c), (B, last - 1))
                    nc.tensor.matmul_mx(out=acc[:, i, columns(c - cols[0], last - cols[0])], lhsT=z_codes[:, rs].bitcast(FP8X4), lhsT_scale=z_planes[:, rs],
                                        rhs=z_codes[:, ms].bitcast(FP8X4), rhs_scale=z_planes[:, ms], start=True, stop=True)
            res = keep.tile([P, n, width], F32, name=over or "res%d_%d" % (rows[0], cols[0]), align_bytes=64)
            if on_scalar:
                nc.scalar.activation(res[:], acc[:], COPY, scale=POOL_SCALE)
            else:
                nc.vector.tensor_scalar(res[:], acc[:], POOL_SCALE, None, MULT)
            nc.sync.dma_start(out[columns(rows[0], rows[1]), cs].rearrange("(i p) n -> p i n", i=n), res[:])

        round_weights(B0)
        for chunk in (B1, A0, A1): round_weights(chunk)
        round_weights(B3, B2)
        for chunk in (A2, A3): round_weights(chunk)
        project(B0)
        project(B1)
        project(A0)
        deal_gates()
        stage_z((B0, B1), tag("w_raw", A0))
        weigh_on_vector(B0)
        project(A1)
        weigh_on_vector(B1)
        stage_z((A0, A1), "z_a01")
        weigh_on_vector(A0)
        project(B3, B2)
        weigh_on_scalar(B3)
        weigh_on_vector(A1)
        project(A2)
        weigh_on_scalar(A2)
        quantise_z(B0, B1)
        quantise_z(A0, A1)
        pool((0, 2), (0, 2), "pool0", True)
        for chunk in (B2, B3, A2, A3): stage_z((chunk,), tag("z_bf", chunk))
        weigh_on_vector(B2)
        project(A3)
        interleave_weighed(B3)
        quantise_z(B2, B2)
        pool((0, 2), (2, 3), "pool1", True)
        quantise_z(B3, B3)
        pool((0, 2), (3, 4), "pool2", True)
        weigh_on_vector(A3)
        interleave_weighed(A2)
        quantise_z(A3, A3)
        quantise_z(A2, A2)
        pool((3, 4), (0, 2), "pool3", True)
        pool((3, 4), (2, 4), "proj0", False)
        pool((2, 3), (0, 2), "proj1", True)
        pool((2, 3), (2, 4), "pool0", False)
